import numpy as np
import ml_dtypes


def mxq(x, axis, fmt="e4m3"):
    dtype, down = {"e4m3": (ml_dtypes.float8_e4m3fn, 7), "e5m2": (ml_dtypes.float8_e5m2, 14)}[fmt]
    v = np.moveaxis(np.asarray(x, np.float32).astype(ml_dtypes.bfloat16).astype(np.float64), axis, -1)
    blocks = v.reshape(v.shape[:-1] + (-1, 32))
    amax = np.abs(blocks).max(-1, keepdims=True)
    byte = np.maximum(np.where(amax > 0, np.frexp(amax)[1] - 1 + 127, 0) - down, 1)
    scale = np.exp2(byte - 127.0)
    codes = (blocks / scale).astype(np.float32).astype(dtype).astype(np.float64)
    return np.moveaxis((codes * scale).reshape(v.shape), -1, axis)


WIDE = False


def mx_kscale(k):
    if not WIDE:
        return np.ones(k)
    levels = np.array([10, -10, 5, -5, 0])
    if k % 512:
        return np.exp2(np.random.permutation(np.resize(levels, k // 32))).repeat(32)
    a = np.empty((k // 512, 16))
    for p in range(k // 512):
        a[p, :8] = np.random.permutation(np.resize(levels, 8))
        for g in range(8):
            far = levels[np.abs(levels - a[p, g]) >= 10]
            a[p, g + 8] = far[np.random.randint(len(far))]
    return np.exp2(a.ravel()).repeat(32)


def f64(x):
    return np.asarray(x).astype(np.float64)


def striped(idx):
    return np.tile(idx.reshape(-1, 16).T, (8, 1)).astype(np.uint16)


def unstriped(offs):
    return offs[:16].T.reshape(-1).astype(np.int64)


def pack_weight(w):
    k, n = w.shape
    w = f64(np.asarray(w, np.float32).astype(ml_dtypes.bfloat16)).reshape(k // 32, 32, n)
    amax = np.abs(w).max(1)
    byte = np.clip(np.where(amax > 0, np.frexp(amax)[1] - 1 + 127 - 7, 1), 1, 254)
    scaled = (w * np.exp2(127.0 - byte)[:, None, :]).reshape(k, n).astype(np.float32)
    words = np.ascontiguousarray(scaled.reshape(k // 512, 128, 4, n).transpose(0, 1, 3, 2)).astype(ml_dtypes.float8_e4m3fn).view(np.uint8)
    return words, np.ascontiguousarray(byte.astype(np.uint8).reshape(k // 512, 16, n))


def unpack_weight(words, scales):
    g, p, n, _ = words.shape
    vals = np.ascontiguousarray(words).view(ml_dtypes.float8_e4m3fn).astype(np.float64) * np.repeat(np.exp2(scales.astype(np.float64) - 127.0), 8, axis=1)[..., None]
    return vals.transpose(0, 1, 3, 2).reshape(g * 512, n)


def planes(y):
    n, m = y.shape
    v = y.astype(np.float32).astype(ml_dtypes.bfloat16).astype(np.float64).reshape(n // 32, 32, m)
    top = np.abs(v).max(1)
    byte = np.clip(np.where(top > 0, np.frexp(top)[1] - 1 + 127 - 7, 1), 1, 254)
    codes = (v * np.exp2(127.0 - byte)[:, None, :]).reshape(n, m).astype(np.float32).astype(ml_dtypes.float8_e4m3fn).view(np.uint8)
    words = codes.reshape(n // 512, 128, 4, m).transpose(0, 1, 3, 2)
    return np.ascontiguousarray(words), np.ascontiguousarray(byte.astype(np.uint8).reshape(n // 512, 16, m))


K, T, S, V, H, N = 512, 2048, 512, 256, 512, 512


def setup_inputs():
    n = np.random.standard_normal
    s = mx_kscale(K)[:, None]
    u = mx_kscale(H)
    near = np.random.permutation(S)
    packed_xT = pack_weight(n((K, T)) * s)
    return {
        "x_words": packed_xT[0],
        "x_scales": packed_xT[1],
        "w1": (n((K, N)) / np.sqrt(K) / s).astype(np.float32),
        "w2": (n((H, N)) / np.sqrt(H) / u[:, None]).astype(np.float32),
        "damp": (np.random.uniform(0.5, 1.0, (H, 1)) * u[:, None]).astype(np.float32),
        "offs": striped(np.random.permutation(T)[:S]),
        "pos1": striped(near[:V]),
        "pos2": striped(near[V:]),
        "pos3": striped(np.random.permutation(S)[:V]),
    }


def reference(x_words, x_scales, w1, w2, damp, offs, pos1, pos2, pos3):
    xq = unpack_weight(x_words, x_scales)[:, unstriped(offs)]
    h = np.tanh(0.5 * ((mxq(f64(w1), 0, "e4m3").T @ xq)))
    z = (h[:, unstriped(pos1)] * h[:, unstriped(pos2)]) * h[:, unstriped(pos3)]
    rr = f64(damp) * (np.log(0.98 * z + 1.0) - np.log(-0.98 * z + 1.0))
    out_0 = mxq(f64(w2), 0, "e4m3").T @ mxq(rr, 0, "e4m3")
    return (out_0,) + planes(out_0)

@@ -1,0 +1,204 @@
+from contextlib import ExitStack
+
+import concourse.mybir as mybir
+
+K, T, S, V, H, N = 512, 2048, 512, 256, 512, 512
+FLOPS = 2 * K * H * S + 2 * H * N * V
+
+F32 = mybir.dt.float32
+BF16 = mybir.dt.bfloat16
+I32 = mybir.dt.int32
+U32 = mybir.dt.uint32
+U16 = mybir.dt.uint16
+U8 = mybir.dt.uint8
+FP8X4 = mybir.dt.float8_e4m3fn_x4
+ACT = mybir.ActivationFunctionType
+ALU = mybir.AluOpType
+
+P = 128
+PACK = 4
+HALF = S // 2
+CHUNK = 128
+
+
+def deal_views(raw, dealt, pair):
+    src = raw[:].rearrange("p j (m t) -> p m j t", t=PACK)[:, :, :, 2 * pair : 2 * pair + 2]
+    dst = dealt[:].rearrange("p t m j -> p m j t")
+    return dst, src
+
+
+def tile_picked_yldpc_bp_po_kernel(
+    tc, x_words, x_scales, w1, w2, damp, offs, pos1, pos2, pos3, out_0, out_1, out_2
+):
+    nc = tc.nc
+    with ExitStack() as ctx:
+        lists = ctx.enter_context(tc.tile_pool(name="lists", bufs=1))
+        keep = ctx.enter_context(tc.tile_pool(name="keep", bufs=1))
+        psum = ctx.enter_context(tc.psum_pool(name="psum", bufs=1))
+
+        offs_t = lists.tile([P, S // 16], U16, name="offs_t")
+        pos_t = [lists.tile([P, V // 16], U16, name="pos_t%d" % d) for d in range(3)]
+
+        x_sc = keep.tile([P, T], U8, name="x_sc", align_bytes=64)
+        x_wd = keep.tile([P, T], U32, name="x_wd", align_bytes=64)
+        w1_raw = keep.tile([P, PACK, H], F32, name="w1_raw", tag="w_raw", align_bytes=64)
+        damp_t = keep.tile([P, PACK], F32, name="damp_t", align_bytes=64)
+
+        nc.vector.memset(x_sc[:].bitcast(I32), 0)
+        nc.sync.dma_start(offs_t[:], offs)
+        nc.sync.dma_start(pos_t[0][:], pos1)
+        nc.sync.dma_start(w1_raw[:], w1.rearrange("(p j) c -> p j c", j=PACK))
+        nc.sync.dma_start(pos_t[1][:], pos2)
+        nc.sync.dma_start(pos_t[2][:], pos3)
+        for q in range(4):
+            nc.sync.dma_start(
+                x_sc[32 * q : 32 * q + 4, :].bitcast(I32), x_scales[0, 4 * q : 4 * q + 4, :].bitcast(I32)
+            )
+        nc.sync.dma_start(x_wd[:].bitcast(I32), x_words[0].rearrange("p n t -> p (n t)").bitcast(I32))
+        nc.gpsimd.dma_start(damp_t[:], damp.rearrange("(p t) o -> p (t o)", t=PACK))
+
+        xg_sc = keep.tile([P, S], U8, name="xg_sc", align_bytes=64)
+        nc.vector.tensor_copy(xg_sc[:], x_sc[:].indirect(offs_t[:]))
+
+        w1_bf = [keep.tile([P, 2, P, PACK], BF16, name="w1_bf%d" % u, align_bytes=64) for u in range(2)]
+        w1_cd = [keep.tile([P, 2 * P], U32, name="w1_cd%d" % u, align_bytes=64) for u in range(2)]
+        w1_sc = [keep.tile([P, 2 * P], U8, name="w1_sc%d" % u, align_bytes=64) for u in range(2)]
+        dst, src = deal_views(w1_raw, w1_bf[0], 0)
+        nc.vector.tensor_copy(dst, src)
+        dst, src = deal_views(w1_raw, w1_bf[1], 1)
+        nc.scalar.activation(dst, src, ACT.Copy)
+        for u in range(2):
+            nc.vector.quantize_mx(
+                out=w1_cd[u][:].bitcast(FP8X4),
+                scales=w1_sc[u][:],
+                in_=w1_bf[u][:].rearrange("p t m j -> p (t m j)"),
+            )
+
+        xg_wd = [keep.tile([P, HALF], U32, name="xg_wd%d" % s, align_bytes=64) for s in range(2)]
+        for s in range(2):
+            cols = HALF // 16
+            nc.vector.tensor_copy(xg_wd[s][:], x_wd[:].indirect(offs_t[:, s * cols : (s + 1) * cols]))
+
+        first = [psum.tile([P, HALF], F32, name="first%d" % s) for s in range(2)]
+        rest = [psum.tile([P, S], F32, name="rest%d" % t) for t in range(1, PACK)]
+        h = [keep.tile([P, S], F32, name="h%d" % t, align_bytes=64) for t in range(PACK)]
+
+        def product1(t, s, out):
+            u, e = divmod(t, 2)
+            nc.tensor.matmul_mx(
+                out=out,
+                lhsT=w1_cd[u][:, e * P : (e + 1) * P].bitcast(FP8X4),
+                lhsT_scale=w1_sc[u][:, e * P : (e + 1) * P],
+                rhs=xg_wd[s][:].bitcast(FP8X4),
+                rhs_scale=xg_sc[:, s * HALF : (s + 1) * HALF],
+                start=True,
+                stop=True,
+            )
+
+        product1(0, 0, first[0][:])
+        nc.scalar.activation(h[0][:, 0:HALF], first[0][:], ACT.Tanh, scale=0.5)
+        product1(1, 0, rest[0][:, 0:HALF])
+        product1(0, 1, first[1][:])
+        nc.scalar.activation(h[0][:, HALF:S], first[1][:], ACT.Tanh, scale=0.5)
+        product1(1, 1, rest[0][:, HALF:S])
+        nc.scalar.activation(h[1][:], rest[0][:], ACT.Tanh, scale=0.5)
+        for t in (2, 3):
+            for s in range(2):
+                product1(t, s, rest[t - 1][:, s * HALF : (s + 1) * HALF])
+            nc.scalar.activation(h[t][:], rest[t - 1][:], ACT.Tanh, scale=0.5)
+
+        w2_raw = keep.tile([P, PACK, N], F32, name="w2_raw", tag="w_raw", align_bytes=64)
+        nc.sync.dma_start(w2_raw[:], w2.rearrange("(p j) c -> p j c", j=PACK))
+        w2_bf = keep.tile([P, PACK, P, PACK], BF16, name="w2_bf", align_bytes=64)
+        w2_cd = keep.tile([P, N], U32, name="w2_cd", align_bytes=64)
+        w2_sc = keep.tile([P, N], U8, name="w2_sc", align_bytes=64)
+        for u in range(2):
+            dst, src = deal_views(w2_raw, w2_bf[:, 2 * u : 2 * u + 2], u)
+            nc.scalar.activation(dst, src, ACT.Copy)
+
+        one = [keep.tile([P, V], F32, name="one%d" % t, align_bytes=64) for t in range(PACK)]
+        two = [keep.tile([P, V], F32, name="two%d" % t, align_bytes=64) for t in range(PACK)]
+        z = [keep.tile([P, 2, V], F32, name="z%d" % u, align_bytes=64) for u in range(2)]
+        up = [keep.tile([P, 2, V], F32, name="up%d" % u, align_bytes=64) for u in range(2)]
+        down = [keep.tile([P, 2, V], F32, name="down%d" % u, align_bytes=64) for u in range(2)]
+        diff = keep.tile([P, PACK, V], F32, name="diff", align_bytes=64)
+        for u in range(2):
+            for t in (2 * u, 2 * u + 1):
+                nc.vector.tensor_copy(one[t][:], h[t][:].indirect(pos_t[0][:]))
+            for t in (2 * u, 2 * u + 1):
+                nc.vector.tensor_tensor(two[t][:], h[t][:].indirect(pos_t[1][:]), one[t][:], ALU.mult)
+            for t in (2 * u, 2 * u + 1):
+                nc.vector.tensor_tensor(z[u][:, t % 2, :], h[t][:].indirect(pos_t[2][:]), two[t][:], ALU.mult)
+
+        nc.scalar.activation(up[0][:], z[0][:], ACT.Ln, scale=0.98, bias=1.0)
+        nc.scalar.activation(down[0][:], z[0][:], ACT.Ln, scale=-0.98, bias=1.0)
+        for e in range(2):
+            nc.scalar.activation(up[1][:, e, :], z[1][:, e, :], ACT.Ln, scale=0.98, bias=1.0)
+            nc.scalar.activation(down[1][:, e, :], z[1][:, e, :], ACT.Ln, scale=-0.98, bias=1.0)
+
+        nc.vector.tensor_tensor(diff[:, 0:2, :], up[0][:], down[0][:], ALU.subtract)
+        nc.vector.tensor_tensor(diff[:, 2:4, :], up[1][:], down[1][:], ALU.subtract)
+
+        y_cd = keep.tile([P, V], U32, name="y_cd", align_bytes=64)
+        y_sc = keep.tile([P, V], U8, name="y_sc", align_bytes=64)
+        out_rows = out_0.rearrange("(p t) v -> p t v", t=PACK)
+        chunks = V // CHUNK
+        spans = [slice(c * CHUNK, (c + 1) * CHUNK) for c in range(chunks)]
+        rr_bf = [keep.tile([P, CHUNK, PACK], BF16, name="rr_bf%d" % c, align_bytes=64) for c in range(chunks)]
+        rr_cd = [keep.tile([P, CHUNK], U32, name="rr_cd%d" % c, align_bytes=64) for c in range(chunks)]
+        rr_sc = [keep.tile([P, CHUNK], U8, name="rr_sc%d" % c, align_bytes=64) for c in range(chunks)]
+        acc = [psum.tile([P, PACK, CHUNK], F32, name="acc%d" % c) for c in range(chunks)]
+        y = [keep.tile([P, PACK, CHUNK], F32, name="y%d" % c, align_bytes=64) for c in range(chunks)]
+        y_bf = [keep.tile([P, CHUNK, PACK], BF16, name="y_bf%d" % c, align_bytes=64) for c in range(chunks)]
+
+        def damped(c):
+            nc.vector.tensor_tensor(
+                rr_bf[c][:].rearrange("p (g i) t -> p g t i", i=4),
+                diff[:, :, spans[c]].rearrange("p t (g i) -> p g t i", i=4),
+                damp_t[:].unsqueeze(1).unsqueeze(3).to_broadcast([P, CHUNK // 4, PACK, 4]),
+                ALU.mult,
+            )
+
+        def product2(c):
+            nc.vector.quantize_mx(
+                out=rr_cd[c][:].bitcast(FP8X4), scales=rr_sc[c][:], in_=rr_bf[c][:].rearrange("p v t -> p (v t)")
+            )
+            for t in range(PACK):
+                nc.tensor.matmul_mx(
+                    out=acc[c][:, t, :],
+                    lhsT=w2_cd[:, t * P : (t + 1) * P].bitcast(FP8X4),
+                    lhsT_scale=w2_sc[:, t * P : (t + 1) * P],
+                    rhs=rr_cd[c][:].bitcast(FP8X4),
+                    rhs_scale=rr_sc[c][:],
+                    start=True,
+                    stop=True,
+                )
+
+        def planes(c):
+            nc.vector.quantize_mx(
+                out=y_cd[:, spans[c]].bitcast(FP8X4),
+                scales=y_sc[:, spans[c]],
+                in_=y_bf[c][:].rearrange("p v t -> p (v t)"),
+            )
+
+        damped(0)
+        nc.vector.quantize_mx(
+            out=w2_cd[:].bitcast(FP8X4), scales=w2_sc[:], in_=w2_bf[:].rearrange("p t m j -> p (t m j)")
+        )
+        product2(0)
+        damped(1)
+        product2(1)
+        nc.scalar.activation(y_bf[0][:], acc[0][:].rearrange("p t v -> p v t"), ACT.Copy)
+        nc.scalar.activation(y[0][:], acc[0][:], ACT.Copy)
+        nc.sync.dma_start(out_rows[:, :, spans[0]], y[0][:])
+        planes(0)
+        nc.vector.tensor_copy(y_bf[1][:], acc[1][:].rearrange("p t v -> p v t"))
+        nc.scalar.activation(y[1][:], acc[1][:], ACT.Copy)
+        nc.sync.dma_start(out_rows[:, :, spans[1]], y[1][:])
+        planes(1)
+        nc.sync.dma_start(out_1[0].rearrange("p n t -> p (n t)").bitcast(I32), y_cd[:].bitcast(I32))
+        for q in range(4):
+            queue = nc.sync if q % 2 else nc.scalar
+            queue.dma_start(
+                out_2[0, 4 * q : 4 * q + 4, :].bitcast(I32), y_sc[32 * q : 32 * q + 4, :].bitcast(I32)
+            )

@@ -44,18 +44,19 @@ def tile_picked_yldpc_bp_po_kernel(
         w1_raw = keep.tile([P, PACK, H], F32, name="w1_raw", tag="w_raw", align_bytes=64)
         damp_t = keep.tile([P, PACK], F32, name="damp_t", align_bytes=64)
 
-        nc.vector.memset(x_sc[:].bitcast(I32), 0)
+        nc.vector.memset(x_sc[:, 0 : T // 2].bitcast(I32), 0)
+        nc.gpsimd.memset(x_sc[:, T // 2 : T].bitcast(I32), 0)
+        nc.sync.dma_start(w1_raw[:], w1.rearrange("(p j) c -> p j c", j=PACK))
         nc.sync.dma_start(offs_t[:], offs)
         nc.sync.dma_start(pos_t[0][:], pos1)
-        nc.sync.dma_start(w1_raw[:], w1.rearrange("(p j) c -> p j c", j=PACK))
-        nc.sync.dma_start(pos_t[1][:], pos2)
-        nc.sync.dma_start(pos_t[2][:], pos3)
         for q in range(4):
             nc.sync.dma_start(
                 x_sc[32 * q : 32 * q + 4, :].bitcast(I32), x_scales[0, 4 * q : 4 * q + 4, :].bitcast(I32)
             )
         nc.sync.dma_start(x_wd[:].bitcast(I32), x_words[0].rearrange("p n t -> p (n t)").bitcast(I32))
-        nc.gpsimd.dma_start(damp_t[:], damp.rearrange("(p t) o -> p (t o)", t=PACK))
+        nc.sync.dma_start(pos_t[1][:], pos2)
+        nc.sync.dma_start(pos_t[2][:], pos3)
+        nc.sync.dma_start(damp_t[:], damp.rearrange("(p t) o -> p (t o)", t=PACK))
 
         xg_sc = keep.tile([P, S], U8, name="xg_sc", align_bytes=64)
         nc.vector.tensor_copy(xg_sc[:], x_sc[:].indirect(offs_t[:]))
@@ -74,13 +75,13 @@ def tile_picked_yldpc_bp_po_kernel(
                 in_=w1_bf[u][:].rearrange("p t m j -> p (t m j)"),
             )
 
-        xg_wd = [keep.tile([P, HALF], U32, name="xg_wd%d" % s, align_bytes=64) for s in range(2)]
+        xg_wd = [keep.tile([P, HALF], U32, name="xg_wd%d" % s, tag="picked%d" % s, align_bytes=64) for s in range(2)]
         for s in range(2):
             cols = HALF // 16
             nc.vector.tensor_copy(xg_wd[s][:], x_wd[:].indirect(offs_t[:, s * cols : (s + 1) * cols]))
 
-        first = [psum.tile([P, HALF], F32, name="first%d" % s) for s in range(2)]
-        rest = [psum.tile([P, S], F32, name="rest%d" % t) for t in range(1, PACK)]
+        first = [psum.tile([P, HALF], F32, name="first%d" % s, tag="bank%d" % s) for s in range(2)]
+        rest = [psum.tile([P, S], F32, name="rest%d" % t, tag="bank%d" % (t + 1)) for t in range(1, PACK)]
         h = [keep.tile([P, S], F32, name="h%d" % t, align_bytes=64) for t in range(PACK)]
 
         def product1(t, s, out):
@@ -107,9 +108,12 @@ def tile_picked_yldpc_bp_po_kernel(
                 product1(t, s, rest[t - 1][:, s * HALF : (s + 1) * HALF])
             nc.scalar.activation(h[t][:], rest[t - 1][:], ACT.Tanh, scale=0.5)
 
+        warm = keep.tile([P, 1], F32, name="warm", align_bytes=64)
+        nc.scalar.activation(warm[:], h[3][:, 0:1], ACT.Ln, scale=0.98, bias=1.0)
+
         w2_raw = keep.tile([P, PACK, N], F32, name="w2_raw", tag="w_raw", align_bytes=64)
         nc.sync.dma_start(w2_raw[:], w2.rearrange("(p j) c -> p j c", j=PACK))
-        w2_bf = keep.tile([P, PACK, P, PACK], BF16, name="w2_bf", align_bytes=64)
+        w2_bf = keep.tile([P, PACK, P, PACK], BF16, name="w2_bf", tag="picked1", align_bytes=64)
         w2_cd = keep.tile([P, N], U32, name="w2_cd", align_bytes=64)
         w2_sc = keep.tile([P, N], U8, name="w2_sc", align_bytes=64)
         for u in range(2):
@@ -119,37 +123,57 @@ def tile_picked_yldpc_bp_po_kernel(
         one = [keep.tile([P, V], F32, name="one%d" % t, align_bytes=64) for t in range(PACK)]
         two = [keep.tile([P, V], F32, name="two%d" % t, align_bytes=64) for t in range(PACK)]
         z = [keep.tile([P, 2, V], F32, name="z%d" % u, align_bytes=64) for u in range(2)]
-        up = [keep.tile([P, 2, V], F32, name="up%d" % u, align_bytes=64) for u in range(2)]
-        down = [keep.tile([P, 2, V], F32, name="down%d" % u, align_bytes=64) for u in range(2)]
+        both_logs = keep.tile([P, 2, PACK, V], F32, name="both_logs", tag="w_raw", align_bytes=64)
+        up = [both_logs[:, 0, 2 * u : 2 * u + 2, :] for u in range(2)]
+        down = [both_logs[:, 1, 2 * u : 2 * u + 2, :] for u in range(2)]
         diff = keep.tile([P, PACK, V], F32, name="diff", align_bytes=64)
-        for u in range(2):
-            for t in (2 * u, 2 * u + 1):
-                nc.vector.tensor_copy(one[t][:], h[t][:].indirect(pos_t[0][:]))
-            for t in (2 * u, 2 * u + 1):
-                nc.vector.tensor_tensor(two[t][:], h[t][:].indirect(pos_t[1][:]), one[t][:], ALU.mult)
-            for t in (2 * u, 2 * u + 1):
-                nc.vector.tensor_tensor(z[u][:, t % 2, :], h[t][:].indirect(pos_t[2][:]), two[t][:], ALU.mult)
+        spans = [slice(c * CHUNK, (c + 1) * CHUNK) for c in range(2)]
+        lists_of = [slice(c * CHUNK // 16, (c + 1) * CHUNK // 16) for c in range(2)]
+        for t in (0, 1):
+            nc.vector.tensor_copy(one[t][:], h[t][:].indirect(pos_t[0][:]))
+        for t in (0, 1):
+            nc.vector.tensor_tensor(two[t][:], h[t][:].indirect(pos_t[1][:]), one[t][:], ALU.mult)
+        for t in (0, 1):
+            nc.vector.tensor_tensor(z[0][:, t, :], h[t][:].indirect(pos_t[2][:]), two[t][:], ALU.mult)
+        for t in (2, 3):
+            nc.vector.tensor_copy(one[t][:], h[t][:].indirect(pos_t[0][:]))
+        for t in (2, 3):
+            nc.vector.tensor_tensor(two[t][:], h[t][:].indirect(pos_t[1][:]), one[t][:], ALU.mult)
+        nc.vector.tensor_tensor(z[1][:, 0, :], h[2][:].indirect(pos_t[2][:]), two[2][:], ALU.mult)
+        for c in range(2):
+            nc.vector.tensor_tensor(
+                z[1][:, 1, spans[c]], h[3][:].indirect(pos_t[2][:, lists_of[c]]), two[3][:, spans[c]], ALU.mult
+            )
 
-        nc.scalar.activation(up[0][:], z[0][:], ACT.Ln, scale=0.98, bias=1.0)
-        nc.scalar.activation(down[0][:], z[0][:], ACT.Ln, scale=-0.98, bias=1.0)
-        for e in range(2):
-            nc.scalar.activation(up[1][:, e, :], z[1][:, e, :], ACT.Ln, scale=0.98, bias=1.0)
-            nc.scalar.activation(down[1][:, e, :], z[1][:, e, :], ACT.Ln, scale=-0.98, bias=1.0)
+        def logs(zs, ups, downs):
+            nc.scalar.activation(ups, zs, ACT.Ln, scale=0.98, bias=1.0)
+            nc.scalar.activation(downs, zs, ACT.Ln, scale=-0.98, bias=1.0)
 
+        logs(z[0][:], up[0][:], down[0][:])
+        logs(z[1][:, 0, :], up[1][:, 0, :], down[1][:, 0, :])
+        for c in range(2):
+            logs(z[1][:, 1, spans[c]], up[1][:, 1, spans[c]], down[1][:, 1, spans[c]])
+
+        nc.vector.quantize_mx(
+            out=w2_cd[:].bitcast(FP8X4), scales=w2_sc[:], in_=w2_bf[:].rearrange("p t m j -> p (t m j)")
+        )
         nc.vector.tensor_tensor(diff[:, 0:2, :], up[0][:], down[0][:], ALU.subtract)
-        nc.vector.tensor_tensor(diff[:, 2:4, :], up[1][:], down[1][:], ALU.subtract)
 
         y_cd = keep.tile([P, V], U32, name="y_cd", align_bytes=64)
         y_sc = keep.tile([P, V], U8, name="y_sc", align_bytes=64)
         out_rows = out_0.rearrange("(p t) v -> p t v", t=PACK)
-        chunks = V // CHUNK
-        spans = [slice(c * CHUNK, (c + 1) * CHUNK) for c in range(chunks)]
-        rr_bf = [keep.tile([P, CHUNK, PACK], BF16, name="rr_bf%d" % c, align_bytes=64) for c in range(chunks)]
-        rr_cd = [keep.tile([P, CHUNK], U32, name="rr_cd%d" % c, align_bytes=64) for c in range(chunks)]
-        rr_sc = [keep.tile([P, CHUNK], U8, name="rr_sc%d" % c, align_bytes=64) for c in range(chunks)]
-        acc = [psum.tile([P, PACK, CHUNK], F32, name="acc%d" % c) for c in range(chunks)]
-        y = [keep.tile([P, PACK, CHUNK], F32, name="y%d" % c, align_bytes=64) for c in range(chunks)]
-        y_bf = [keep.tile([P, CHUNK, PACK], BF16, name="y_bf%d" % c, align_bytes=64) for c in range(chunks)]
+        rr_bf = [keep.tile([P, CHUNK, PACK], BF16, name="rr_bf%d" % c, align_bytes=64) for c in range(2)]
+        rr_cd = [keep.tile([P, CHUNK], U32, name="rr_cd%d" % c, align_bytes=64) for c in range(2)]
+        rr_sc = [keep.tile([P, CHUNK], U8, name="rr_sc%d" % c, align_bytes=64) for c in range(2)]
+        acc = [
+            [psum.tile([P, 2, CHUNK], F32, name="acc%d%d" % (c, u), tag="bank%d" % ((5 + 2 * c + u) % 8)) for u in range(2)]
+            for c in range(2)
+        ]
+        y = [keep.tile([P, PACK, CHUNK], F32, name="y%d" % c, align_bytes=64) for c in range(2)]
+        y_bf = [keep.tile([P, CHUNK, PACK], BF16, name="y_bf%d" % c, align_bytes=64) for c in range(2)]
+
+        def subtract(c):
+            nc.vector.tensor_tensor(diff[:, 2:4, spans[c]], up[1][:, :, spans[c]], down[1][:, :, spans[c]], ALU.subtract)
 
         def damped(c):
             nc.vector.tensor_tensor(
@@ -164,8 +188,9 @@ def tile_picked_yldpc_bp_po_kernel(
                 out=rr_cd[c][:].bitcast(FP8X4), scales=rr_sc[c][:], in_=rr_bf[c][:].rearrange("p v t -> p (v t)")
             )
             for t in range(PACK):
+                u, e = divmod(t, 2)
                 nc.tensor.matmul_mx(
-                    out=acc[c][:, t, :],
+                    out=acc[c][u][:, e, :],
                     lhsT=w2_cd[:, t * P : (t + 1) * P].bitcast(FP8X4),
                     lhsT_scale=w2_sc[:, t * P : (t + 1) * P],
                     rhs=rr_cd[c][:].bitcast(FP8X4),
@@ -173,28 +198,27 @@ def tile_picked_yldpc_bp_po_kernel(
                     start=True,
                     stop=True,
                 )
+                if e:
+                    nc.scalar.activation(y[c][:, 2 * u : 2 * u + 2, :], acc[c][u][:], ACT.Copy)
+            nc.sync.dma_start(out_rows[:, :, spans[c]], y[c][:])
 
         def planes(c):
+            nc.vector.tensor_copy(
+                y_bf[c][:].rearrange("p (g i) t -> p g t i", i=4), y[c][:].rearrange("p t (g i) -> p g t i", i=4)
+            )
             nc.vector.quantize_mx(
                 out=y_cd[:, spans[c]].bitcast(FP8X4),
                 scales=y_sc[:, spans[c]],
                 in_=y_bf[c][:].rearrange("p v t -> p (v t)"),
             )
 
+        subtract(0)
         damped(0)
-        nc.vector.quantize_mx(
-            out=w2_cd[:].bitcast(FP8X4), scales=w2_sc[:], in_=w2_bf[:].rearrange("p t m j -> p (t m j)")
-        )
         product2(0)
+        subtract(1)
         damped(1)
         product2(1)
-        nc.scalar.activation(y_bf[0][:], acc[0][:].rearrange("p t v -> p v t"), ACT.Copy)
-        nc.scalar.activation(y[0][:], acc[0][:], ACT.Copy)
-        nc.sync.dma_start(out_rows[:, :, spans[0]], y[0][:])
         planes(0)
-        nc.vector.tensor_copy(y_bf[1][:], acc[1][:].rearrange("p t v -> p v t"))
-        nc.scalar.activation(y[1][:], acc[1][:], ACT.Copy)
-        nc.sync.dma_start(out_rows[:, :, spans[1]], y[1][:])
         planes(1)
         nc.sync.dma_start(out_1[0].rearrange("p n t -> p (n t)").bitcast(I32), y_cd[:].bitcast(I32))
         for q in range(4):

@@ -54,6 +54,9 @@ def tile_picked_yldpc_bp_po_kernel(
                 x_sc[32 * q : 32 * q + 4, :].bitcast(I32), x_scales[0, 4 * q : 4 * q + 4, :].bitcast(I32)
             )
         nc.sync.dma_start(x_wd[:].bitcast(I32), x_words[0].rearrange("p n t -> p (n t)").bitcast(I32))
+        w2_rows = w2.rearrange("(p j) c -> p j c", j=PACK)
+        w2_early = keep.tile([P, PACK, N // 2], F32, name="w2_early", align_bytes=64)
+        nc.sync.dma_start(w2_early[:], w2_rows[:, :, 0 : N // 2])
         nc.sync.dma_start(pos_t[1][:], pos2)
         nc.sync.dma_start(pos_t[2][:], pos3)
         nc.sync.dma_start(damp_t[:], damp.rearrange("(p t) o -> p (t o)", t=PACK))
@@ -80,7 +83,14 @@ def tile_picked_yldpc_bp_po_kernel(
             cols = HALF // 16
             nc.vector.tensor_copy(xg_wd[s][:], x_wd[:].indirect(offs_t[:, s * cols : (s + 1) * cols]))
 
-        first = [psum.tile([P, HALF], F32, name="first%d" % s, tag="bank%d" % s) for s in range(2)]
+        w2_bf = keep.tile([P, PACK, P, PACK], BF16, name="w2_bf", align_bytes=64)
+        nc.vector.tensor_copy(
+            w2_bf[:, :, 0 : P // 2, :].rearrange("p t m j -> p m j t"),
+            w2_early[:].rearrange("p j (m t) -> p m j t", t=PACK),
+        )
+
+        first = [psum.tile([P, HALF], F32, name="first", tag="bank0")]
+        last = [psum.tile([P, CHUNK], F32, name="last%d" % c, tag=("bank1", "bank5")[c]) for c in range(2)]
         rest = [psum.tile([P, S], F32, name="rest%d" % t, tag="bank%d" % (t + 1)) for t in range(1, PACK)]
         h = [keep.tile([P, S], F32, name="h%d" % t, align_bytes=64) for t in range(PACK)]
 
@@ -99,8 +109,18 @@ def tile_picked_yldpc_bp_po_kernel(
         product1(0, 0, first[0][:])
         nc.scalar.activation(h[0][:, 0:HALF], first[0][:], ACT.Tanh, scale=0.5)
         product1(1, 0, rest[0][:, 0:HALF])
-        product1(0, 1, first[1][:])
-        nc.scalar.activation(h[0][:, HALF:S], first[1][:], ACT.Tanh, scale=0.5)
+        for c in range(2):
+            lo = HALF + c * CHUNK
+            nc.tensor.matmul_mx(
+                out=last[c][:],
+                lhsT=w1_cd[0][:, 0:P].bitcast(FP8X4),
+                lhsT_scale=w1_sc[0][:, 0:P],
+                rhs=xg_wd[1][:, c * CHUNK : (c + 1) * CHUNK].bitcast(FP8X4),
+                rhs_scale=xg_sc[:, lo : lo + CHUNK],
+                start=True,
+                stop=True,
+            )
+            nc.scalar.activation(h[0][:, lo : lo + CHUNK], last[c][:], ACT.Tanh, scale=0.5)
         product1(1, 1, rest[0][:, HALF:S])
         nc.scalar.activation(h[1][:], rest[0][:], ACT.Tanh, scale=0.5)
         for t in (2, 3):
@@ -111,14 +131,15 @@ def tile_picked_yldpc_bp_po_kernel(
         warm = keep.tile([P, 1], F32, name="warm", align_bytes=64)
         nc.scalar.activation(warm[:], h[3][:, 0:1], ACT.Ln, scale=0.98, bias=1.0)
 
-        w2_raw = keep.tile([P, PACK, N], F32, name="w2_raw", tag="w_raw", align_bytes=64)
-        nc.sync.dma_start(w2_raw[:], w2.rearrange("(p j) c -> p j c", j=PACK))
-        w2_bf = keep.tile([P, PACK, P, PACK], BF16, name="w2_bf", tag="picked1", align_bytes=64)
+        w2_raw = keep.tile([P, PACK, N // 2], F32, name="w2_raw", tag="w_raw", align_bytes=64)
+        nc.sync.dma_start(w2_raw[:], w2_rows[:, :, N // 2 : N])
         w2_cd = keep.tile([P, N], U32, name="w2_cd", align_bytes=64)
         w2_sc = keep.tile([P, N], U8, name="w2_sc", align_bytes=64)
-        for u in range(2):
-            dst, src = deal_views(w2_raw, w2_bf[:, 2 * u : 2 * u + 2], u)
-            nc.scalar.activation(dst, src, ACT.Copy)
+        nc.scalar.activation(
+            w2_bf[:, :, P // 2 : P, :].rearrange("p t m j -> p m j t"),
+            w2_raw[:].rearrange("p j (m t) -> p m j t", t=PACK),
+            ACT.Copy,
+        )
 
         one = [keep.tile([P, V], F32, name="one%d" % t, align_bytes=64) for t in range(PACK)]
         two = [keep.tile([P, V], F32, name="two%d" % t, align_bytes=64) for t in range(PACK)]
@@ -126,38 +147,66 @@ def tile_picked_yldpc_bp_po_kernel(
         both_logs = keep.tile([P, 2, PACK, V], F32, name="both_logs", tag="w_raw", align_bytes=64)
         up = [both_logs[:, 0, 2 * u : 2 * u + 2, :] for u in range(2)]
         down = [both_logs[:, 1, 2 * u : 2 * u + 2, :] for u in range(2)]
-        diff = keep.tile([P, PACK, V], F32, name="diff", align_bytes=64)
+        diff = keep.tile([P, PACK, CHUNK], F32, name="diff", align_bytes=64)
         spans = [slice(c * CHUNK, (c + 1) * CHUNK) for c in range(2)]
         lists_of = [slice(c * CHUNK // 16, (c + 1) * CHUNK // 16) for c in range(2)]
-        for t in (0, 1):
-            nc.vector.tensor_copy(one[t][:], h[t][:].indirect(pos_t[0][:]))
-        for t in (0, 1):
-            nc.vector.tensor_tensor(two[t][:], h[t][:].indirect(pos_t[1][:]), one[t][:], ALU.mult)
-        for t in (0, 1):
-            nc.vector.tensor_tensor(z[0][:, t, :], h[t][:].indirect(pos_t[2][:]), two[t][:], ALU.mult)
-        for t in (2, 3):
-            nc.vector.tensor_copy(one[t][:], h[t][:].indirect(pos_t[0][:]))
-        for t in (2, 3):
-            nc.vector.tensor_tensor(two[t][:], h[t][:].indirect(pos_t[1][:]), one[t][:], ALU.mult)
-        nc.vector.tensor_tensor(z[1][:, 0, :], h[2][:].indirect(pos_t[2][:]), two[2][:], ALU.mult)
-        for c in range(2):
-            nc.vector.tensor_tensor(
-                z[1][:, 1, spans[c]], h[3][:].indirect(pos_t[2][:, lists_of[c]]), two[3][:, spans[c]], ALU.mult
-            )
+        whole = [(slice(0, V), slice(0, V // 16))]
+        halves = list(zip(spans, lists_of))
+
+        def first_factor(t, pieces):
+            for cols, entries in pieces:
+                nc.vector.tensor_copy(one[t][:, cols], h[t][:].indirect(pos_t[0][:, entries]))
+
+        def second_factor(t, pieces):
+            for cols, entries in pieces:
+                nc.vector.tensor_tensor(
+                    two[t][:, cols], h[t][:].indirect(pos_t[1][:, entries]), one[t][:, cols], ALU.mult
+                )
+
+        def third_factor(t, pieces):
+            for cols, entries in pieces:
+                nc.vector.tensor_tensor(
+                    z[t // 2][:, t % 2, cols], h[t][:].indirect(pos_t[2][:, entries]), two[t][:, cols], ALU.mult
+                )
+
+        first_factor(0, halves)
+        first_factor(1, whole)
+        second_factor(0, halves)
+        second_factor(1, whole)
+        third_factor(0, whole)
+        third_factor(1, whole)
+        first_factor(2, whole)
+        first_factor(3, whole)
+        second_factor(2, whole)
+        second_factor(3, halves[:1])
+        third_factor(2, whole)
+        second_factor(3, halves[1:])
+        third_factor(3, halves)
 
         def logs(zs, ups, downs):
             nc.scalar.activation(ups, zs, ACT.Ln, scale=0.98, bias=1.0)
             nc.scalar.activation(downs, zs, ACT.Ln, scale=-0.98, bias=1.0)
 
-        logs(z[0][:], up[0][:], down[0][:])
-        logs(z[1][:, 0, :], up[1][:, 0, :], down[1][:, 0, :])
-        for c in range(2):
-            logs(z[1][:, 1, spans[c]], up[1][:, 1, spans[c]], down[1][:, 1, spans[c]])
+        damped_logs = keep.tile([P, 2, PACK, CHUNK], F32, name="damped_logs", align_bytes=64)
+
+        def damp_logs(t):
+            nc.scalar.activation(
+                damped_logs[:, :, t, :], both_logs[:, :, t, spans[0]], ACT.Copy, scale=damp_t[:, t : t + 1]
+            )
+
+        for e in range(2):
+            logs(z[0][:, e, :], up[0][:, e, :], down[0][:, e, :])
+        damp_logs(0)
+        damp_logs(1)
+        logs(z[1][:, 0, spans[0]], up[1][:, 0, spans[0]], down[1][:, 0, spans[0]])
+        logs(z[1][:, 1, spans[0]], up[1][:, 1, spans[0]], down[1][:, 1, spans[0]])
+        damp_logs(2)
+        damp_logs(3)
+        logs(z[1][:, :, spans[1]], up[1][:, :, spans[1]], down[1][:, :, spans[1]])
 
         nc.vector.quantize_mx(
             out=w2_cd[:].bitcast(FP8X4), scales=w2_sc[:], in_=w2_bf[:].rearrange("p t m j -> p (t m j)")
         )
-        nc.vector.tensor_tensor(diff[:, 0:2, :], up[0][:], down[0][:], ALU.subtract)
 
         y_cd = keep.tile([P, V], U32, name="y_cd", align_bytes=64)
         y_sc = keep.tile([P, V], U8, name="y_sc", align_bytes=64)
@@ -172,54 +221,66 @@ def tile_picked_yldpc_bp_po_kernel(
         y = [keep.tile([P, PACK, CHUNK], F32, name="y%d" % c, align_bytes=64) for c in range(2)]
         y_bf = [keep.tile([P, CHUNK, PACK], BF16, name="y_bf%d" % c, align_bytes=64) for c in range(2)]
 
-        def subtract(c):
-            nc.vector.tensor_tensor(diff[:, 2:4, spans[c]], up[1][:, :, spans[c]], down[1][:, :, spans[c]], ALU.subtract)
+        def by_fours(ap):
+            return ap.rearrange("p t (g i) -> p g t i", i=4)
 
-        def damped(c):
-            nc.vector.tensor_tensor(
-                rr_bf[c][:].rearrange("p (g i) t -> p g t i", i=4),
-                diff[:, :, spans[c]].rearrange("p t (g i) -> p g t i", i=4),
-                damp_t[:].unsqueeze(1).unsqueeze(3).to_broadcast([P, CHUNK // 4, PACK, 4]),
-                ALU.mult,
-            )
+        def woven(ap):
+            return ap.rearrange("p (g i) t -> p g t i", i=4)
 
-        def product2(c):
+        def quantise_rr(c):
             nc.vector.quantize_mx(
                 out=rr_cd[c][:].bitcast(FP8X4), scales=rr_sc[c][:], in_=rr_bf[c][:].rearrange("p v t -> p (v t)")
             )
+
+        def product2(c, t, out):
+            nc.tensor.matmul_mx(
+                out=out,
+                lhsT=w2_cd[:, t * P : (t + 1) * P].bitcast(FP8X4),
+                lhsT_scale=w2_sc[:, t * P : (t + 1) * P],
+                rhs=rr_cd[c][:].bitcast(FP8X4),
+                rhs_scale=rr_sc[c][:],
+                start=True,
+                stop=True,
+            )
+
+        def chunk_out(c):
             for t in range(PACK):
                 u, e = divmod(t, 2)
-                nc.tensor.matmul_mx(
-                    out=acc[c][u][:, e, :],
-                    lhsT=w2_cd[:, t * P : (t + 1) * P].bitcast(FP8X4),
-                    lhsT_scale=w2_sc[:, t * P : (t + 1) * P],
-                    rhs=rr_cd[c][:].bitcast(FP8X4),
-                    rhs_scale=rr_sc[c][:],
-                    start=True,
-                    stop=True,
-                )
+                product2(c, t, acc[c][u][:, e, :])
                 if e:
                     nc.scalar.activation(y[c][:, 2 * u : 2 * u + 2, :], acc[c][u][:], ACT.Copy)
             nc.sync.dma_start(out_rows[:, :, spans[c]], y[c][:])
 
-        def planes(c):
-            nc.vector.tensor_copy(
-                y_bf[c][:].rearrange("p (g i) t -> p g t i", i=4), y[c][:].rearrange("p t (g i) -> p g t i", i=4)
-            )
+        def quantise_y(c):
             nc.vector.quantize_mx(
                 out=y_cd[:, spans[c]].bitcast(FP8X4),
                 scales=y_sc[:, spans[c]],
                 in_=y_bf[c][:].rearrange("p v t -> p (v t)"),
             )
 
-        subtract(0)
-        damped(0)
-        product2(0)
-        subtract(1)
-        damped(1)
-        product2(1)
-        planes(0)
-        planes(1)
+        def subtract(groups):
+            nc.vector.tensor_tensor(
+                diff[:, groups, :], both_logs[:, 0, groups, spans[1]], both_logs[:, 1, groups, spans[1]], ALU.subtract
+            )
+
+        subtract(slice(0, 2))
+        nc.vector.tensor_tensor(
+            woven(rr_bf[0][:]), by_fours(damped_logs[:, 0]), by_fours(damped_logs[:, 1]), ALU.subtract
+        )
+        subtract(slice(2, 4))
+        quantise_rr(0)
+        chunk_out(0)
+        nc.vector.tensor_tensor(
+            woven(rr_bf[1][:]),
+            by_fours(diff[:]),
+            damp_t[:].unsqueeze(1).unsqueeze(3).to_broadcast([P, CHUNK // 4, PACK, 4]),
+            ALU.mult,
+        )
+        quantise_rr(1)
+        chunk_out(1)
+        for c in range(2):
+            nc.vector.tensor_copy(woven(y_bf[c][:]), by_fours(y[c][:]))
+            quantise_y(c)
         nc.sync.dma_start(out_1[0].rearrange("p n t -> p (n t)").bitcast(I32), y_cd[:].bitcast(I32))
         for q in range(4):
             queue = nc.sync if q % 2 else nc.scalar

@@ -49,10 +49,9 @@ def tile_picked_yldpc_bp_po_kernel(
         nc.sync.dma_start(w1_raw[:], w1.rearrange("(p j) c -> p j c", j=PACK))
         nc.sync.dma_start(offs_t[:], offs)
         nc.sync.dma_start(pos_t[0][:], pos1)
-        for q in range(4):
-            nc.sync.dma_start(
-                x_sc[32 * q : 32 * q + 4, :].bitcast(I32), x_scales[0, 4 * q : 4 * q + 4, :].bitcast(I32)
-            )
+        scale_rows = x_scales[0].rearrange("(q r) c -> r q c", r=4)
+        for r in range(4):
+            nc.sync.dma_start(x_sc[r:P:32, :].bitcast(I32), scale_rows[r].bitcast(I32))
         nc.sync.dma_start(x_wd[:].bitcast(I32), x_words[0].rearrange("p n t -> p (n t)").bitcast(I32))
         w2_rows = w2.rearrange("(p j) c -> p j c", j=PACK)
         w2_early = keep.tile([P, PACK, N // 2], F32, name="w2_early", align_bytes=64)

@@ -17,14 +17,28 @@ ALU = mybir.AluOpType
 
 P = 128
 PACK = 4
+STRIPE = 16
 HALF = S // 2
-CHUNK = 128
+QUARTER = S // 4
+CHUNK = V // 2
+SLOPE = 0.98
 
 
-def deal_views(raw, dealt, pair):
+def dealt_pair(raw, dealt, pair):
     src = raw[:].rearrange("p j (m t) -> p m j t", t=PACK)[:, :, :, 2 * pair : 2 * pair + 2]
-    dst = dealt[:].rearrange("p t m j -> p m j t")
-    return dst, src
+    return dealt[:].rearrange("p t m j -> p m j t"), src
+
+
+def dealt_all(raw, dealt):
+    return dealt.rearrange("p t m j -> p m j t"), raw[:].rearrange("p j (m t) -> p m j t", t=PACK)
+
+
+def by_fours(grouped):
+    return grouped.rearrange("p t (g i) -> p g t i", i=4)
+
+
+def woven(tile):
+    return tile.rearrange("p (g i) t -> p g t i", i=4)
 
 
 def tile_picked_yldpc_bp_po_kernel(
@@ -36,13 +50,33 @@ def tile_picked_yldpc_bp_po_kernel(
         keep = ctx.enter_context(tc.tile_pool(name="keep", bufs=1))
         psum = ctx.enter_context(tc.psum_pool(name="psum", bufs=1))
 
-        offs_t = lists.tile([P, S // 16], U16, name="offs_t")
-        pos_t = [lists.tile([P, V // 16], U16, name="pos_t%d" % d) for d in range(3)]
+        def sbuf(name, shape, dtype, tag=""):
+            return keep.tile(shape, dtype, name=name, tag=tag or name, align_bytes=64)
 
-        x_sc = keep.tile([P, T], U8, name="x_sc", align_bytes=64)
-        x_wd = keep.tile([P, T], U32, name="x_wd", align_bytes=64)
-        w1_raw = keep.tile([P, PACK, H], F32, name="w1_raw", tag="w_raw", align_bytes=64)
-        damp_t = keep.tile([P, PACK], F32, name="damp_t", align_bytes=64)
+        def bank(name, shape, number):
+            return psum.tile(shape, F32, name=name, tag="bank%d" % number)
+
+        def quantise(codes, scales, values):
+            nc.vector.quantize_mx(out=codes.bitcast(FP8X4), scales=scales, in_=values)
+
+        def product(out, w_codes, w_scales, codes, scales):
+            nc.tensor.matmul_mx(
+                out=out,
+                lhsT=w_codes.bitcast(FP8X4),
+                lhsT_scale=w_scales,
+                rhs=codes.bitcast(FP8X4),
+                rhs_scale=scales,
+                start=True,
+                stop=True,
+            )
+
+        offs_t = lists.tile([P, S // STRIPE], U16, name="offs_t")
+        pos_t = [lists.tile([P, V // STRIPE], U16, name="pos_t%d" % d) for d in range(3)]
+
+        x_sc = sbuf("x_sc", [P, T], U8)
+        x_wd = sbuf("x_wd", [P, T], U32)
+        w1_raw = sbuf("w1_raw", [P, PACK, H], F32, tag="staging")
+        damp_t = sbuf("damp_t", [P, PACK], F32)
 
         nc.vector.memset(x_sc[:, 0 : T // 2].bitcast(I32), 0)
         nc.gpsimd.memset(x_sc[:, T // 2 : T].bitcast(I32), 0)
@@ -54,221 +88,167 @@ def tile_picked_yldpc_bp_po_kernel(
             nc.sync.dma_start(x_sc[r:P:32, :].bitcast(I32), scale_rows[r].bitcast(I32))
         nc.sync.dma_start(x_wd[:].bitcast(I32), x_words[0].rearrange("p n t -> p (n t)").bitcast(I32))
         w2_rows = w2.rearrange("(p j) c -> p j c", j=PACK)
-        w2_early = keep.tile([P, PACK, N // 2], F32, name="w2_early", align_bytes=64)
+        w2_early = sbuf("w2_early", [P, PACK, N // 2], F32)
         nc.sync.dma_start(w2_early[:], w2_rows[:, :, 0 : N // 2])
         nc.sync.dma_start(pos_t[1][:], pos2)
         nc.sync.dma_start(pos_t[2][:], pos3)
         nc.sync.dma_start(damp_t[:], damp.rearrange("(p t) o -> p (t o)", t=PACK))
 
-        xg_sc = keep.tile([P, S], U8, name="xg_sc", align_bytes=64)
+        xg_sc = sbuf("xg_sc", [P, S], U8)
         nc.vector.tensor_copy(xg_sc[:], x_sc[:].indirect(offs_t[:]))
 
-        w1_bf = [keep.tile([P, 2, P, PACK], BF16, name="w1_bf%d" % u, align_bytes=64) for u in range(2)]
-        w1_cd = [keep.tile([P, 2 * P], U32, name="w1_cd%d" % u, align_bytes=64) for u in range(2)]
-        w1_sc = [keep.tile([P, 2 * P], U8, name="w1_sc%d" % u, align_bytes=64) for u in range(2)]
-        dst, src = deal_views(w1_raw, w1_bf[0], 0)
-        nc.vector.tensor_copy(dst, src)
-        dst, src = deal_views(w1_raw, w1_bf[1], 1)
-        nc.scalar.activation(dst, src, ACT.Copy)
+        w1_bf = [sbuf("w1_bf%d" % u, [P, 2, P, PACK], BF16) for u in range(2)]
+        w1_cd = [sbuf("w1_cd%d" % u, [P, 2 * P], U32) for u in range(2)]
+        w1_sc = [sbuf("w1_sc%d" % u, [P, 2 * P], U8) for u in range(2)]
+        nc.vector.tensor_copy(*dealt_pair(w1_raw, w1_bf[0], 0))
+        nc.scalar.activation(*dealt_pair(w1_raw, w1_bf[1], 1), ACT.Copy)
         for u in range(2):
-            nc.vector.quantize_mx(
-                out=w1_cd[u][:].bitcast(FP8X4),
-                scales=w1_sc[u][:],
-                in_=w1_bf[u][:].rearrange("p t m j -> p (t m j)"),
-            )
+            quantise(w1_cd[u][:], w1_sc[u][:], w1_bf[u][:].rearrange("p t m j -> p (t m j)"))
 
-        xg_wd = [keep.tile([P, HALF], U32, name="xg_wd%d" % s, tag="picked%d" % s, align_bytes=64) for s in range(2)]
+        xg_wd = [sbuf("xg_wd%d" % s, [P, HALF], U32) for s in range(2)]
         for s in range(2):
-            cols = HALF // 16
-            nc.vector.tensor_copy(xg_wd[s][:], x_wd[:].indirect(offs_t[:, s * cols : (s + 1) * cols]))
+            entries = slice(s * HALF // STRIPE, (s + 1) * HALF // STRIPE)
+            nc.vector.tensor_copy(xg_wd[s][:], x_wd[:].indirect(offs_t[:, entries]))
 
-        w2_bf = keep.tile([P, PACK, P, PACK], BF16, name="w2_bf", align_bytes=64)
-        nc.vector.tensor_copy(
-            w2_bf[:, :, 0 : P // 2, :].rearrange("p t m j -> p m j t"),
-            w2_early[:].rearrange("p j (m t) -> p m j t", t=PACK),
-        )
+        w2_bf = sbuf("w2_bf", [P, PACK, P, PACK], BF16)
+        nc.vector.tensor_copy(*dealt_all(w2_early, w2_bf[:, :, 0 : P // 2, :]))
 
-        first = [psum.tile([P, HALF], F32, name="first", tag="bank0")]
-        last = [psum.tile([P, CHUNK], F32, name="last%d" % c, tag=("bank1", "bank5")[c]) for c in range(2)]
-        rest = [psum.tile([P, S], F32, name="rest%d" % t, tag="bank%d" % (t + 1)) for t in range(1, PACK)]
-        h = [keep.tile([P, S], F32, name="h%d" % t, align_bytes=64) for t in range(PACK)]
+        head = bank("head", [P, HALF], 0)
+        ends = [bank("end%d" % k, [P, QUARTER], number) for k, number in enumerate((1, 5))]
+        rest = [bank("rest%d" % t, [P, S], t + 1) for t in range(1, PACK)]
+        h = [sbuf("h%d" % t, [P, S], F32) for t in range(PACK)]
 
-        def product1(t, s, out):
+        def product1(out, t, first, width):
             u, e = divmod(t, 2)
-            nc.tensor.matmul_mx(
-                out=out,
-                lhsT=w1_cd[u][:, e * P : (e + 1) * P].bitcast(FP8X4),
-                lhsT_scale=w1_sc[u][:, e * P : (e + 1) * P],
-                rhs=xg_wd[s][:].bitcast(FP8X4),
-                rhs_scale=xg_sc[:, s * HALF : (s + 1) * HALF],
-                start=True,
-                stop=True,
+            s, inside = divmod(first, HALF)
+            group = slice(e * P, (e + 1) * P)
+            product(
+                out,
+                w1_cd[u][:, group],
+                w1_sc[u][:, group],
+                xg_wd[s][:, inside : inside + width],
+                xg_sc[:, first : first + width],
             )
 
-        product1(0, 0, first[0][:])
-        nc.scalar.activation(h[0][:, 0:HALF], first[0][:], ACT.Tanh, scale=0.5)
-        product1(1, 0, rest[0][:, 0:HALF])
-        for c in range(2):
-            lo = HALF + c * CHUNK
-            nc.tensor.matmul_mx(
-                out=last[c][:],
-                lhsT=w1_cd[0][:, 0:P].bitcast(FP8X4),
-                lhsT_scale=w1_sc[0][:, 0:P],
-                rhs=xg_wd[1][:, c * CHUNK : (c + 1) * CHUNK].bitcast(FP8X4),
-                rhs_scale=xg_sc[:, lo : lo + CHUNK],
-                start=True,
-                stop=True,
-            )
-            nc.scalar.activation(h[0][:, lo : lo + CHUNK], last[c][:], ACT.Tanh, scale=0.5)
-        product1(1, 1, rest[0][:, HALF:S])
-        nc.scalar.activation(h[1][:], rest[0][:], ACT.Tanh, scale=0.5)
+        def tanh_half(out, sums):
+            nc.scalar.activation(out, sums, ACT.Tanh, scale=0.5)
+
+        product1(head[:], 0, 0, HALF)
+        tanh_half(h[0][:, 0:HALF], head[:])
+        product1(rest[0][:, 0:HALF], 1, 0, HALF)
+        for k in range(2):
+            first = HALF + k * QUARTER
+            product1(ends[k][:], 0, first, QUARTER)
+            tanh_half(h[0][:, first : first + QUARTER], ends[k][:])
+        product1(rest[0][:, HALF:S], 1, HALF, HALF)
+        tanh_half(h[1][:], rest[0][:])
         for t in (2, 3):
-            for s in range(2):
-                product1(t, s, rest[t - 1][:, s * HALF : (s + 1) * HALF])
-            nc.scalar.activation(h[t][:], rest[t - 1][:], ACT.Tanh, scale=0.5)
+            for first in (0, HALF):
+                product1(rest[t - 1][:, first : first + HALF], t, first, HALF)
+            tanh_half(h[t][:], rest[t - 1][:])
 
-        warm = keep.tile([P, 1], F32, name="warm", align_bytes=64)
-        nc.scalar.activation(warm[:], h[3][:, 0:1], ACT.Ln, scale=0.98, bias=1.0)
+        warm = sbuf("warm", [P, 1], F32)
+        nc.scalar.activation(warm[:], h[PACK - 1][:, 0:1], ACT.Ln, scale=SLOPE, bias=1.0)
 
-        w2_raw = keep.tile([P, PACK, N // 2], F32, name="w2_raw", tag="w_raw", align_bytes=64)
-        nc.sync.dma_start(w2_raw[:], w2_rows[:, :, N // 2 : N])
-        w2_cd = keep.tile([P, N], U32, name="w2_cd", align_bytes=64)
-        w2_sc = keep.tile([P, N], U8, name="w2_sc", align_bytes=64)
-        nc.scalar.activation(
-            w2_bf[:, :, P // 2 : P, :].rearrange("p t m j -> p m j t"),
-            w2_raw[:].rearrange("p j (m t) -> p m j t", t=PACK),
-            ACT.Copy,
-        )
+        w2_late = sbuf("w2_late", [P, PACK, N // 2], F32, tag="staging")
+        nc.sync.dma_start(w2_late[:], w2_rows[:, :, N // 2 : N])
+        w2_cd = sbuf("w2_cd", [P, N], U32)
+        w2_sc = sbuf("w2_sc", [P, N], U8)
+        nc.scalar.activation(*dealt_all(w2_late, w2_bf[:, :, P // 2 : P, :]), ACT.Copy)
 
-        one = [keep.tile([P, V], F32, name="one%d" % t, align_bytes=64) for t in range(PACK)]
-        two = [keep.tile([P, V], F32, name="two%d" % t, align_bytes=64) for t in range(PACK)]
-        z = [keep.tile([P, 2, V], F32, name="z%d" % u, align_bytes=64) for u in range(2)]
-        both_logs = keep.tile([P, 2, PACK, V], F32, name="both_logs", tag="w_raw", align_bytes=64)
-        up = [both_logs[:, 0, 2 * u : 2 * u + 2, :] for u in range(2)]
-        down = [both_logs[:, 1, 2 * u : 2 * u + 2, :] for u in range(2)]
-        diff = keep.tile([P, PACK, CHUNK], F32, name="diff", align_bytes=64)
-        spans = [slice(c * CHUNK, (c + 1) * CHUNK) for c in range(2)]
-        lists_of = [slice(c * CHUNK // 16, (c + 1) * CHUNK // 16) for c in range(2)]
-        whole = [(slice(0, V), slice(0, V // 16))]
-        halves = list(zip(spans, lists_of))
+        one = [sbuf("one%d" % t, [P, V], F32) for t in range(PACK)]
+        two = [sbuf("two%d" % t, [P, V], F32) for t in range(PACK)]
+        z = [sbuf("z%d" % u, [P, 2, V], F32) for u in range(2)]
+        logs = sbuf("logs", [P, 2, PACK, V], F32, tag="staging")
+        diff = sbuf("diff", [P, PACK, CHUNK], F32)
+        chunks = [slice(c * CHUNK, (c + 1) * CHUNK) for c in range(2)]
+        both = slice(0, V)
 
-        def first_factor(t, pieces):
-            for cols, entries in pieces:
-                nc.vector.tensor_copy(one[t][:, cols], h[t][:].indirect(pos_t[0][:, entries]))
+        def picked(t, d, nodes):
+            return h[t][:].indirect(pos_t[d][:, nodes.start // STRIPE : nodes.stop // STRIPE])
 
-        def second_factor(t, pieces):
-            for cols, entries in pieces:
-                nc.vector.tensor_tensor(
-                    two[t][:, cols], h[t][:].indirect(pos_t[1][:, entries]), one[t][:, cols], ALU.mult
-                )
+        def factor1(t, nodes):
+            nc.vector.tensor_copy(one[t][:, nodes], picked(t, 0, nodes))
 
-        def third_factor(t, pieces):
-            for cols, entries in pieces:
-                nc.vector.tensor_tensor(
-                    z[t // 2][:, t % 2, cols], h[t][:].indirect(pos_t[2][:, entries]), two[t][:, cols], ALU.mult
-                )
+        def factor2(t, nodes):
+            nc.vector.tensor_tensor(two[t][:, nodes], picked(t, 1, nodes), one[t][:, nodes], ALU.mult)
 
-        first_factor(0, halves)
-        first_factor(1, whole)
-        second_factor(0, halves)
-        second_factor(1, whole)
-        third_factor(0, whole)
-        third_factor(1, whole)
-        first_factor(2, whole)
-        first_factor(3, whole)
-        second_factor(2, whole)
-        second_factor(3, halves[:1])
-        third_factor(2, whole)
-        second_factor(3, halves[1:])
-        third_factor(3, halves)
+        def factor3(t, nodes):
+            nc.vector.tensor_tensor(z[t // 2][:, t % 2, nodes], picked(t, 2, nodes), two[t][:, nodes], ALU.mult)
 
-        def logs(zs, ups, downs):
-            nc.scalar.activation(ups, zs, ACT.Ln, scale=0.98, bias=1.0)
-            nc.scalar.activation(downs, zs, ACT.Ln, scale=-0.98, bias=1.0)
+        for factor in (factor1, factor2):
+            for nodes in chunks:
+                factor(0, nodes)
+            factor(1, both)
+        for t in (0, 1):
+            factor3(t, both)
+        for t in (2, 3):
+            factor1(t, both)
+        factor2(2, both)
+        for nodes in chunks:
+            factor2(3, nodes)
+            factor3(2, nodes)
+            factor3(3, nodes)
 
-        damped_logs = keep.tile([P, 2, PACK, CHUNK], F32, name="damped_logs", align_bytes=64)
+        def take_logs(groups, nodes):
+            u = groups.start // 2
+            zs = z[u][:, groups.start - 2 * u : groups.stop - 2 * u, nodes]
+            nc.scalar.activation(logs[:, 0, groups, nodes], zs, ACT.Ln, scale=SLOPE, bias=1.0)
+            nc.scalar.activation(logs[:, 1, groups, nodes], zs, ACT.Ln, scale=-SLOPE, bias=1.0)
+
+        damped_logs = sbuf("damped_logs", [P, 2, PACK, CHUNK], F32)
 
         def damp_logs(t):
             nc.scalar.activation(
-                damped_logs[:, :, t, :], both_logs[:, :, t, spans[0]], ACT.Copy, scale=damp_t[:, t : t + 1]
+                damped_logs[:, :, t, :], logs[:, :, t, chunks[0]], ACT.Copy, scale=damp_t[:, t : t + 1]
             )
 
-        for e in range(2):
-            logs(z[0][:, e, :], up[0][:, e, :], down[0][:, e, :])
-        damp_logs(0)
-        damp_logs(1)
-        logs(z[1][:, 0, spans[0]], up[1][:, 0, spans[0]], down[1][:, 0, spans[0]])
-        logs(z[1][:, 1, spans[0]], up[1][:, 1, spans[0]], down[1][:, 1, spans[0]])
-        damp_logs(2)
-        damp_logs(3)
-        logs(z[1][:, :, spans[1]], up[1][:, :, spans[1]], down[1][:, :, spans[1]])
+        for pair, nodes in (((0, 1), both), ((2, 3), chunks[0])):
+            for t in pair:
+                take_logs(slice(t, t + 1), nodes)
+            for t in pair:
+                damp_logs(t)
+        take_logs(slice(2, 4), chunks[1])
 
-        nc.vector.quantize_mx(
-            out=w2_cd[:].bitcast(FP8X4), scales=w2_sc[:], in_=w2_bf[:].rearrange("p t m j -> p (t m j)")
-        )
+        quantise(w2_cd[:], w2_sc[:], w2_bf[:].rearrange("p t m j -> p (t m j)"))
 
-        y_cd = keep.tile([P, V], U32, name="y_cd", align_bytes=64)
-        y_sc = keep.tile([P, V], U8, name="y_sc", align_bytes=64)
+        y_cd = sbuf("y_cd", [P, V], U32)
+        y_sc = sbuf("y_sc", [P, V], U8)
         out_rows = out_0.rearrange("(p t) v -> p t v", t=PACK)
-        rr_bf = [keep.tile([P, CHUNK, PACK], BF16, name="rr_bf%d" % c, align_bytes=64) for c in range(2)]
-        rr_cd = [keep.tile([P, CHUNK], U32, name="rr_cd%d" % c, align_bytes=64) for c in range(2)]
-        rr_sc = [keep.tile([P, CHUNK], U8, name="rr_sc%d" % c, align_bytes=64) for c in range(2)]
+        rr_bf = [sbuf("rr_bf%d" % c, [P, CHUNK, PACK], BF16) for c in range(2)]
+        rr_cd = [sbuf("rr_cd%d" % c, [P, CHUNK], U32) for c in range(2)]
+        rr_sc = [sbuf("rr_sc%d" % c, [P, CHUNK], U8) for c in range(2)]
         acc = [
-            [psum.tile([P, 2, CHUNK], F32, name="acc%d%d" % (c, u), tag="bank%d" % ((5 + 2 * c + u) % 8)) for u in range(2)]
-            for c in range(2)
+            [bank("acc%d%d" % (c, u), [P, 2, CHUNK], number) for u, number in enumerate(numbers)]
+            for c, numbers in enumerate(((5, 6), (7, 0)))
         ]
-        y = [keep.tile([P, PACK, CHUNK], F32, name="y%d" % c, align_bytes=64) for c in range(2)]
-        y_bf = [keep.tile([P, CHUNK, PACK], BF16, name="y_bf%d" % c, align_bytes=64) for c in range(2)]
-
-        def by_fours(ap):
-            return ap.rearrange("p t (g i) -> p g t i", i=4)
-
-        def woven(ap):
-            return ap.rearrange("p (g i) t -> p g t i", i=4)
-
-        def quantise_rr(c):
-            nc.vector.quantize_mx(
-                out=rr_cd[c][:].bitcast(FP8X4), scales=rr_sc[c][:], in_=rr_bf[c][:].rearrange("p v t -> p (v t)")
-            )
-
-        def product2(c, t, out):
-            nc.tensor.matmul_mx(
-                out=out,
-                lhsT=w2_cd[:, t * P : (t + 1) * P].bitcast(FP8X4),
-                lhsT_scale=w2_sc[:, t * P : (t + 1) * P],
-                rhs=rr_cd[c][:].bitcast(FP8X4),
-                rhs_scale=rr_sc[c][:],
-                start=True,
-                stop=True,
-            )
-
-        def chunk_out(c):
-            for t in range(PACK):
-                u, e = divmod(t, 2)
-                product2(c, t, acc[c][u][:, e, :])
-                if e:
-                    nc.scalar.activation(y[c][:, 2 * u : 2 * u + 2, :], acc[c][u][:], ACT.Copy)
-            nc.sync.dma_start(out_rows[:, :, spans[c]], y[c][:])
-
-        def quantise_y(c):
-            nc.vector.quantize_mx(
-                out=y_cd[:, spans[c]].bitcast(FP8X4),
-                scales=y_sc[:, spans[c]],
-                in_=y_bf[c][:].rearrange("p v t -> p (v t)"),
-            )
+        y = [sbuf("y%d" % c, [P, PACK, CHUNK], F32) for c in range(2)]
+        y_bf = [sbuf("y_bf%d" % c, [P, CHUNK, PACK], BF16) for c in range(2)]
+        pairs = [slice(0, 2), slice(2, 4)]
 
         def subtract(groups):
             nc.vector.tensor_tensor(
-                diff[:, groups, :], both_logs[:, 0, groups, spans[1]], both_logs[:, 1, groups, spans[1]], ALU.subtract
+                diff[:, groups, :], logs[:, 0, groups, chunks[1]], logs[:, 1, groups, chunks[1]], ALU.subtract
             )
 
-        subtract(slice(0, 2))
+        def quantise_rr(c):
+            quantise(rr_cd[c][:], rr_sc[c][:], rr_bf[c][:].rearrange("p v t -> p (v t)"))
+
+        def product2(c, u):
+            for e in range(2):
+                group = slice((2 * u + e) * P, (2 * u + e + 1) * P)
+                product(acc[c][u][:, e, :], w2_cd[:, group], w2_sc[:, group], rr_cd[c][:], rr_sc[c][:])
+            nc.scalar.activation(y[c][:, pairs[u], :], acc[c][u][:], ACT.Copy)
+
+        subtract(pairs[0])
         nc.vector.tensor_tensor(
             woven(rr_bf[0][:]), by_fours(damped_logs[:, 0]), by_fours(damped_logs[:, 1]), ALU.subtract
         )
-        subtract(slice(2, 4))
+        subtract(pairs[1])
         quantise_rr(0)
-        chunk_out(0)
+        for u in range(2):
+            product2(0, u)
+        nc.sync.dma_start(out_rows[:, :, chunks[0]], y[0][:])
         nc.vector.tensor_tensor(
             woven(rr_bf[1][:]),
             by_fours(diff[:]),
@@ -276,10 +256,13 @@ def tile_picked_yldpc_bp_po_kernel(
             ALU.mult,
         )
         quantise_rr(1)
-        chunk_out(1)
+        for u in range(2):
+            product2(1, u)
+            nc.sync.dma_start(out_rows[:, pairs[u], chunks[1]], y[1][:, pairs[u], :])
+
         for c in range(2):
             nc.vector.tensor_copy(woven(y_bf[c][:]), by_fours(y[c][:]))
-            quantise_y(c)
+            quantise(y_cd[:, chunks[c]], y_sc[:, chunks[c]], y_bf[c][:].rearrange("p v t -> p (v t)"))
         nc.sync.dma_start(out_1[0].rearrange("p n t -> p (n t)").bitcast(I32), y_cd[:].bitcast(I32))
         for q in range(4):
             queue = nc.sync if q % 2 else nc.scalar

@@ -258,7 +258,7 @@ def tile_picked_yldpc_bp_po_kernel(
         quantise_rr(1)
         for u in range(2):
             product2(1, u)
-            nc.sync.dma_start(out_rows[:, pairs[u], chunks[1]], y[1][:, pairs[u], :])
+        nc.sync.dma_start(out_rows[:, :, chunks[1]], y[1][:])
 
         for c in range(2):
             nc.vector.tensor_copy(woven(y_bf[c][:]), by_fours(y[c][:]))

@@ -154,7 +154,14 @@ def tile_picked_yldpc_bp_po_kernel(
         nc.sync.dma_start(w2_late[:], w2_rows[:, :, N // 2 : N])
         w2_cd = sbuf("w2_cd", [P, N], U32)
         w2_sc = sbuf("w2_sc", [P, N], U8)
-        nc.scalar.activation(*dealt_all(w2_late, w2_bf[:, :, P // 2 : P, :]), ACT.Copy)
+        nc.gpsimd.tensor_scalar(
+            w2_bf[:, :, P // 2 : P, :],
+            w2_late[:].rearrange("p j (m t) -> p t m j", t=PACK),
+            1.0,
+            0.0,
+            ALU.mult,
+            ALU.add,
+        )
 
         one = [sbuf("one%d" % t, [P, V], F32) for t in range(PACK)]
         two = [sbuf("two%d" % t, [P, V], F32) for t in range(PACK)]
@@ -176,14 +183,11 @@ def tile_picked_yldpc_bp_po_kernel(
         def factor3(t, nodes):
             nc.vector.tensor_tensor(z[t // 2][:, t % 2, nodes], picked(t, 2, nodes), two[t][:, nodes], ALU.mult)
 
-        for factor in (factor1, factor2):
-            for nodes in chunks:
-                factor(0, nodes)
-            factor(1, both)
-        for t in (0, 1):
-            factor3(t, both)
-        for t in (2, 3):
+        for t in range(PACK):
             factor1(t, both)
+        for factor in (factor2, factor3):
+            for t in (0, 1):
+                factor(t, both)
         factor2(2, both)
         for nodes in chunks:
             factor2(3, nodes)

@@ -164,10 +164,8 @@ def tile_picked_yldpc_bp_po_kernel(
         )
 
         one = [sbuf("one%d" % t, [P, V], F32) for t in range(PACK)]
-        two = [sbuf("two%d" % t, [P, V], F32) for t in range(PACK)]
+        two = [sbuf("two%d" % t, [P, V], F32) for t in range(2)]
         z = [sbuf("z%d" % u, [P, 2, V], F32) for u in range(2)]
-        logs = sbuf("logs", [P, 2, PACK, V], F32, tag="staging")
-        diff = sbuf("diff", [P, PACK, CHUNK], F32)
         chunks = [slice(c * CHUNK, (c + 1) * CHUNK) for c in range(2)]
         both = slice(0, V)
 
@@ -183,36 +181,32 @@ def tile_picked_yldpc_bp_po_kernel(
         def factor3(t, nodes):
             nc.vector.tensor_tensor(z[t // 2][:, t % 2, nodes], picked(t, 2, nodes), two[t][:, nodes], ALU.mult)
 
-        for t in range(PACK):
-            factor1(t, both)
-        for factor in (factor2, factor3):
+        for factor in (factor1, factor2, factor3):
             for t in (0, 1):
                 factor(t, both)
-        factor2(2, both)
+        for t in (2, 3):
+            factor1(t, both)
         for nodes in chunks:
-            factor2(3, nodes)
-            factor3(2, nodes)
-            factor3(3, nodes)
+            part = [sbuf("part%d_%d" % (t, nodes.start), [P, CHUNK], F32, tag="part%d" % t) for t in (2, 3)]
+            for t in (2, 3):
+                nc.vector.tensor_tensor(part[t - 2][:], picked(t, 1, nodes), one[t][:, nodes], ALU.mult)
+            for t in (2, 3):
+                nc.vector.tensor_tensor(z[1][:, t - 2, nodes], picked(t, 2, nodes), part[t - 2][:], ALU.mult)
 
-        def take_logs(groups, nodes):
-            u = groups.start // 2
-            zs = z[u][:, groups.start - 2 * u : groups.stop - 2 * u, nodes]
-            nc.scalar.activation(logs[:, 0, groups, nodes], zs, ACT.Ln, scale=SLOPE, bias=1.0)
-            nc.scalar.activation(logs[:, 1, groups, nodes], zs, ACT.Ln, scale=-SLOPE, bias=1.0)
+        def take_logs(t, nodes):
+            width = nodes.stop - nodes.start
+            logs = sbuf("logs%d_%d" % (t, nodes.start), [P, 2, width], F32, tag="logs%d" % t)
+            zs = z[t // 2][:, t % 2, nodes]
+            nc.scalar.activation(logs[:, 0, :], zs, ACT.Ln, scale=SLOPE, bias=1.0)
+            nc.scalar.activation(logs[:, 1, :], zs, ACT.Ln, scale=-SLOPE, bias=1.0)
+            return logs
 
-        damped_logs = sbuf("damped_logs", [P, 2, PACK, CHUNK], F32)
+        damped_logs = sbuf("damped_logs", [P, 2, PACK, V], F32)
 
-        def damp_logs(t):
-            nc.scalar.activation(
-                damped_logs[:, :, t, :], logs[:, :, t, chunks[0]], ACT.Copy, scale=damp_t[:, t : t + 1]
-            )
-
-        for pair, nodes in (((0, 1), both), ((2, 3), chunks[0])):
-            for t in pair:
-                take_logs(slice(t, t + 1), nodes)
-            for t in pair:
-                damp_logs(t)
-        take_logs(slice(2, 4), chunks[1])
+        for pair, nodes in (((0, 1), both), ((2, 3), chunks[0]), ((2, 3), chunks[1])):
+            taken = [take_logs(t, nodes) for t in pair]
+            for t, logs in zip(pair, taken):
+                nc.scalar.activation(damped_logs[:, :, t, nodes], logs[:], ACT.Copy, scale=damp_t[:, t : t + 1])
 
         quantise(w2_cd[:], w2_sc[:], w2_bf[:].rearrange("p t m j -> p (t m j)"))
 
@@ -230,9 +224,12 @@ def tile_picked_yldpc_bp_po_kernel(
         y_bf = [sbuf("y_bf%d" % c, [P, CHUNK, PACK], BF16) for c in range(2)]
         pairs = [slice(0, 2), slice(2, 4)]
 
-        def subtract(groups):
+        def subtract(c):
             nc.vector.tensor_tensor(
-                diff[:, groups, :], logs[:, 0, groups, chunks[1]], logs[:, 1, groups, chunks[1]], ALU.subtract
+                woven(rr_bf[c][:]),
+                by_fours(damped_logs[:, 0, :, chunks[c]]),
+                by_fours(damped_logs[:, 1, :, chunks[c]]),
+                ALU.subtract,
             )
 
         def quantise_rr(c):
@@ -244,25 +241,12 @@ def tile_picked_yldpc_bp_po_kernel(
                 product(acc[c][u][:, e, :], w2_cd[:, group], w2_sc[:, group], rr_cd[c][:], rr_sc[c][:])
             nc.scalar.activation(y[c][:, pairs[u], :], acc[c][u][:], ACT.Copy)
 
-        subtract(pairs[0])
-        nc.vector.tensor_tensor(
-            woven(rr_bf[0][:]), by_fours(damped_logs[:, 0]), by_fours(damped_logs[:, 1]), ALU.subtract
-        )
-        subtract(pairs[1])
-        quantise_rr(0)
-        for u in range(2):
-            product2(0, u)
-        nc.sync.dma_start(out_rows[:, :, chunks[0]], y[0][:])
-        nc.vector.tensor_tensor(
-            woven(rr_bf[1][:]),
-            by_fours(diff[:]),
-            damp_t[:].unsqueeze(1).unsqueeze(3).to_broadcast([P, CHUNK // 4, PACK, 4]),
-            ALU.mult,
-        )
-        quantise_rr(1)
-        for u in range(2):
-            product2(1, u)
-        nc.sync.dma_start(out_rows[:, :, chunks[1]], y[1][:])
+        for c in range(2):
+            subtract(c)
+            quantise_rr(c)
+            for u in range(2):
+                product2(c, u)
+            nc.sync.dma_start(out_rows[:, :, chunks[c]], y[c][:])
 
         for c in range(2):
             nc.vector.tensor_copy(woven(y_bf[c][:]), by_fours(y[c][:]))

@@ -152,8 +152,6 @@ def tile_picked_yldpc_bp_po_kernel(
 
         w2_late = sbuf("w2_late", [P, PACK, N // 2], F32, tag="staging")
         nc.sync.dma_start(w2_late[:], w2_rows[:, :, N // 2 : N])
-        w2_cd = sbuf("w2_cd", [P, N], U32)
-        w2_sc = sbuf("w2_sc", [P, N], U8)
         nc.gpsimd.tensor_scalar(
             w2_bf[:, :, P // 2 : P, :],
             w2_late[:].rearrange("p j (m t) -> p t m j", t=PACK),
@@ -181,11 +179,12 @@ def tile_picked_yldpc_bp_po_kernel(
         def factor3(t, nodes):
             nc.vector.tensor_tensor(z[t // 2][:, t % 2, nodes], picked(t, 2, nodes), two[t][:, nodes], ALU.mult)
 
-        for factor in (factor1, factor2, factor3):
+        for t in (0, 1, 2):
+            factor1(t, both)
+        for factor in (factor2, factor3):
             for t in (0, 1):
                 factor(t, both)
-        for t in (2, 3):
-            factor1(t, both)
+        factor1(3, both)
         for nodes in chunks:
             part = [sbuf("part%d_%d" % (t, nodes.start), [P, CHUNK], F32, tag="part%d" % t) for t in (2, 3)]
             for t in (2, 3):
@@ -193,22 +192,31 @@ def tile_picked_yldpc_bp_po_kernel(
             for t in (2, 3):
                 nc.vector.tensor_tensor(z[1][:, t - 2, nodes], picked(t, 2, nodes), part[t - 2][:], ALU.mult)
 
-        def take_logs(t, nodes):
-            width = nodes.stop - nodes.start
-            logs = sbuf("logs%d_%d" % (t, nodes.start), [P, 2, width], F32, tag="logs%d" % t)
+        def take_logs(t, nodes, logs):
             zs = z[t // 2][:, t % 2, nodes]
             nc.scalar.activation(logs[:, 0, :], zs, ACT.Ln, scale=SLOPE, bias=1.0)
             nc.scalar.activation(logs[:, 1, :], zs, ACT.Ln, scale=-SLOPE, bias=1.0)
-            return logs
 
-        damped_logs = sbuf("damped_logs", [P, 2, PACK, V], F32)
+        damped = [sbuf("damped%d" % c, [P, 2, PACK, CHUNK], F32) for c in range(2)]
 
-        for pair, nodes in (((0, 1), both), ((2, 3), chunks[0]), ((2, 3), chunks[1])):
-            taken = [take_logs(t, nodes) for t in pair]
-            for t, logs in zip(pair, taken):
-                nc.scalar.activation(damped_logs[:, :, t, nodes], logs[:], ACT.Copy, scale=damp_t[:, t : t + 1])
+        def damp_logs(c, t, logs):
+            nc.scalar.activation(damped[c][:, :, t, :], logs, ACT.Copy, scale=damp_t[:, t : t + 1])
 
-        quantise(w2_cd[:], w2_sc[:], w2_bf[:].rearrange("p t m j -> p (t m j)"))
+        logs = [sbuf("logs%d" % t, [P, 2, V if t < 2 else CHUNK], F32) for t in range(PACK)]
+        for t in (0, 1):
+            take_logs(t, both, logs[t])
+        for c in range(2):
+            for t in (0, 1):
+                damp_logs(c, t, logs[t][:, :, chunks[c]])
+        for t in (2, 3):
+            take_logs(t, chunks[0], logs[t])
+        for t in (2, 3):
+            damp_logs(0, t, logs[t][:])
+        last_logs = sbuf("last_logs", [P, 2, 2, CHUNK], F32, tag="logs2")
+        for t in (2, 3):
+            take_logs(t, chunks[1], last_logs[:, t - 2])
+        for t in (2, 3):
+            damp_logs(1, t, last_logs[:, t - 2])
 
         y_cd = sbuf("y_cd", [P, V], U32)
         y_sc = sbuf("y_sc", [P, V], U8)
@@ -216,10 +224,6 @@ def tile_picked_yldpc_bp_po_kernel(
         rr_bf = [sbuf("rr_bf%d" % c, [P, CHUNK, PACK], BF16) for c in range(2)]
         rr_cd = [sbuf("rr_cd%d" % c, [P, CHUNK], U32) for c in range(2)]
         rr_sc = [sbuf("rr_sc%d" % c, [P, CHUNK], U8) for c in range(2)]
-        acc = [
-            [bank("acc%d%d" % (c, u), [P, 2, CHUNK], number) for u, number in enumerate(numbers)]
-            for c, numbers in enumerate(((5, 6), (7, 0)))
-        ]
         y = [sbuf("y%d" % c, [P, PACK, CHUNK], F32) for c in range(2)]
         y_bf = [sbuf("y_bf%d" % c, [P, CHUNK, PACK], BF16) for c in range(2)]
         pairs = [slice(0, 2), slice(2, 4)]
@@ -227,25 +231,38 @@ def tile_picked_yldpc_bp_po_kernel(
         def subtract(c):
             nc.vector.tensor_tensor(
                 woven(rr_bf[c][:]),
-                by_fours(damped_logs[:, 0, :, chunks[c]]),
-                by_fours(damped_logs[:, 1, :, chunks[c]]),
+                by_fours(damped[c][:, 0]),
+                by_fours(damped[c][:, 1]),
                 ALU.subtract,
             )
 
         def quantise_rr(c):
             quantise(rr_cd[c][:], rr_sc[c][:], rr_bf[c][:].rearrange("p v t -> p (v t)"))
 
-        def product2(c, u):
-            for e in range(2):
-                group = slice((2 * u + e) * P, (2 * u + e + 1) * P)
-                product(acc[c][u][:, e, :], w2_cd[:, group], w2_sc[:, group], rr_cd[c][:], rr_sc[c][:])
-            nc.scalar.activation(y[c][:, pairs[u], :], acc[c][u][:], ACT.Copy)
+        def product2(c, groups, number, leave):
+            sums = bank("acc%d%d" % (c, groups.start), [P, groups.stop - groups.start, CHUNK], number)
+            for t in range(groups.start, groups.stop):
+                group = slice(t * P, (t + 1) * P)
+                product(sums[:, t - groups.start, :], w2_cd[:, group], w2_sc[:, group], rr_cd[c][:], rr_sc[c][:])
+            leave(y[c][:, groups, :], sums[:])
 
+        def by_scalar(out, sums):
+            nc.scalar.activation(out, sums, ACT.Copy)
+
+        ways_out = [
+            [(pairs[0], 5, by_scalar), (pairs[1], 6, by_scalar)],
+            [(pairs[0], 7, nc.vector.tensor_copy), (slice(2, 3), 0, by_scalar), (slice(3, 4), 1, by_scalar)],
+        ]
+        subtract(0)
+        w2_cd = sbuf("w2_cd", [P, N], U32)
+        w2_sc = sbuf("w2_sc", [P, N], U8, tag="logs3")
+        quantise(w2_cd[:], w2_sc[:], w2_bf[:].rearrange("p t m j -> p (t m j)"))
         for c in range(2):
-            subtract(c)
+            if c:
+                subtract(c)
             quantise_rr(c)
-            for u in range(2):
-                product2(c, u)
+            for way in ways_out[c]:
+                product2(c, *way)
             nc.sync.dma_start(out_rows[:, :, chunks[c]], y[c][:])
 
         for c in range(2):

@@ -78,11 +78,10 @@ def tile_picked_yldpc_bp_po_kernel(
         w1_raw = sbuf("w1_raw", [P, PACK, H], F32, tag="staging")
         damp_t = sbuf("damp_t", [P, PACK], F32)
 
-        nc.vector.memset(x_sc[:, 0 : T // 2].bitcast(I32), 0)
-        nc.gpsimd.memset(x_sc[:, T // 2 : T].bitcast(I32), 0)
+        nc.vector.memset(x_sc[:, 0 : 3 * T // 4].bitcast(I32), 0)
+        nc.gpsimd.memset(x_sc[:, 3 * T // 4 : T].bitcast(I32), 0)
         nc.sync.dma_start(w1_raw[:], w1.rearrange("(p j) c -> p j c", j=PACK))
         nc.sync.dma_start(offs_t[:], offs)
-        nc.sync.dma_start(pos_t[0][:], pos1)
         scale_rows = x_scales[0].rearrange("(q r) c -> r q c", r=4)
         for r in range(4):
             nc.sync.dma_start(x_sc[r:P:32, :].bitcast(I32), scale_rows[r].bitcast(I32))
@@ -90,6 +89,7 @@ def tile_picked_yldpc_bp_po_kernel(
         w2_rows = w2.rearrange("(p j) c -> p j c", j=PACK)
         w2_early = sbuf("w2_early", [P, PACK, N // 2], F32)
         nc.sync.dma_start(w2_early[:], w2_rows[:, :, 0 : N // 2])
+        nc.sync.dma_start(pos_t[0][:], pos1)
         nc.sync.dma_start(pos_t[1][:], pos2)
         nc.sync.dma_start(pos_t[2][:], pos3)
         nc.sync.dma_start(damp_t[:], damp.rearrange("(p t) o -> p (t o)", t=PACK))
@@ -153,8 +153,8 @@ def tile_picked_yldpc_bp_po_kernel(
         w2_late = sbuf("w2_late", [P, PACK, N // 2], F32, tag="staging")
         nc.sync.dma_start(w2_late[:], w2_rows[:, :, N // 2 : N])
         nc.gpsimd.tensor_scalar(
-            w2_bf[:, :, P // 2 : P, :],
-            w2_late[:].rearrange("p j (m t) -> p t m j", t=PACK),
+            w2_bf[:, :, P // 2 : P, :].rearrange("p t m j -> p m t j"),
+            w2_late[:].rearrange("p j (m t) -> p m t j", t=PACK),
             1.0,
             0.0,
             ALU.mult,
@@ -268,7 +268,9 @@ def tile_picked_yldpc_bp_po_kernel(
         for c in range(2):
             nc.vector.tensor_copy(woven(y_bf[c][:]), by_fours(y[c][:]))
             quantise(y_cd[:, chunks[c]], y_sc[:, chunks[c]], y_bf[c][:].rearrange("p v t -> p (v t)"))
-        nc.sync.dma_start(out_1[0].rearrange("p n t -> p (n t)").bitcast(I32), y_cd[:].bitcast(I32))
+        out_words = out_1[0].rearrange("p n t -> p (n t)").bitcast(I32)
+        for c, queue in enumerate((nc.scalar, nc.sync)):
+            queue.dma_start(out_words[:, chunks[c]], y_cd[:, chunks[c]].bitcast(I32))
         for q in range(4):
             queue = nc.sync if q % 2 else nc.scalar
             queue.dma_start(

@@ -147,9 +147,6 @@ def tile_picked_yldpc_bp_po_kernel(
                 product1(rest[t - 1][:, first : first + HALF], t, first, HALF)
             tanh_half(h[t][:], rest[t - 1][:])
 
-        warm = sbuf("warm", [P, 1], F32)
-        nc.scalar.activation(warm[:], h[PACK - 1][:, 0:1], ACT.Ln, scale=SLOPE, bias=1.0)
-
         w2_late = sbuf("w2_late", [P, PACK, N // 2], F32, tag="staging")
         nc.sync.dma_start(w2_late[:], w2_rows[:, :, N // 2 : N])
         nc.gpsimd.tensor_scalar(
@@ -171,7 +168,10 @@ def tile_picked_yldpc_bp_po_kernel(
             return h[t][:].indirect(pos_t[d][:, nodes.start // STRIPE : nodes.stop // STRIPE])
 
         def factor1(t, nodes):
-            nc.vector.tensor_copy(one[t][:, nodes], picked(t, 0, nodes))
+            if t < 2:
+                nc.vector.tensor_copy(one[t][:, nodes], picked(t, 0, nodes))
+            else:
+                nc.scalar.activation(one[t][:, nodes], picked(t, 0, nodes), ACT.Copy)
 
         def factor2(t, nodes):
             nc.vector.tensor_tensor(two[t][:, nodes], picked(t, 1, nodes), one[t][:, nodes], ALU.mult)
@@ -179,12 +179,11 @@ def tile_picked_yldpc_bp_po_kernel(
         def factor3(t, nodes):
             nc.vector.tensor_tensor(z[t // 2][:, t % 2, nodes], picked(t, 2, nodes), two[t][:, nodes], ALU.mult)
 
-        for t in (0, 1, 2):
+        for t in range(PACK):
             factor1(t, both)
         for factor in (factor2, factor3):
             for t in (0, 1):
                 factor(t, both)
-        factor1(3, both)
         for nodes in chunks:
             part = [sbuf("part%d_%d" % (t, nodes.start), [P, CHUNK], F32, tag="part%d" % t) for t in (2, 3)]
             for t in (2, 3):
@@ -200,7 +199,10 @@ def tile_picked_yldpc_bp_po_kernel(
         damped = [sbuf("damped%d" % c, [P, 2, PACK, CHUNK], F32) for c in range(2)]
 
         def damp_logs(c, t, logs):
-            nc.scalar.activation(damped[c][:, :, t, :], logs, ACT.Copy, scale=damp_t[:, t : t + 1])
+            if t < 2:
+                nc.vector.tensor_scalar(damped[c][:, :, t, :], logs, damp_t[:, t : t + 1], None, ALU.mult)
+            else:
+                nc.scalar.activation(damped[c][:, :, t, :], logs, ACT.Copy, scale=damp_t[:, t : t + 1])
 
         logs = [sbuf("logs%d" % t, [P, 2, V if t < 2 else CHUNK], F32) for t in range(PACK)]
         for t in (0, 1):

@@ -98,20 +98,26 @@ def tile_picked_yldpc_bp_po_kernel(
         nc.vector.tensor_copy(xg_sc[:], x_sc[:].indirect(offs_t[:]))
 
         w1_bf = [sbuf("w1_bf%d" % u, [P, 2, P, PACK], BF16) for u in range(2)]
-        w1_cd = [sbuf("w1_cd%d" % u, [P, 2 * P], U32) for u in range(2)]
-        w1_sc = [sbuf("w1_sc%d" % u, [P, 2 * P], U8) for u in range(2)]
+        w1_cd = [sbuf("w1_cd%d" % u, [P, 2 * P], U32, tag=tag) for u, tag in enumerate(("", "x_wd"))]
+        w1_planes = sbuf("w1_planes", [P, PACK * P], U8, tag="x_sc")
+        w1_sc = [w1_planes[:, 2 * P * u : 2 * P * (u + 1)] for u in range(2)]
         nc.vector.tensor_copy(*dealt_pair(w1_raw, w1_bf[0], 0))
         nc.scalar.activation(*dealt_pair(w1_raw, w1_bf[1], 1), ACT.Copy)
-        for u in range(2):
-            quantise(w1_cd[u][:], w1_sc[u][:], w1_bf[u][:].rearrange("p t m j -> p (t m j)"))
+
+        def quantise_w1(u):
+            quantise(w1_cd[u][:], w1_sc[u], w1_bf[u][:].rearrange("p t m j -> p (t m j)"))
+
+        quantise_w1(0)
 
         xg_wd = [sbuf("xg_wd%d" % s, [P, HALF], U32) for s in range(2)]
-        for s in range(2):
-            entries = slice(s * HALF // STRIPE, (s + 1) * HALF // STRIPE)
-            nc.vector.tensor_copy(xg_wd[s][:], x_wd[:].indirect(offs_t[:, entries]))
+        for first, width in ((0, HALF), (HALF, QUARTER), (HALF + QUARTER, QUARTER)):
+            entries = slice(first // STRIPE, (first + width) // STRIPE)
+            s, inside = divmod(first, HALF)
+            nc.vector.tensor_copy(xg_wd[s][:, inside : inside + width], x_wd[:].indirect(offs_t[:, entries]))
 
         w2_bf = sbuf("w2_bf", [P, PACK, P, PACK], BF16)
         nc.vector.tensor_copy(*dealt_all(w2_early, w2_bf[:, :, 0 : P // 2, :]))
+        quantise_w1(1)
 
         head = bank("head", [P, HALF], 0)
         ends = [bank("end%d" % k, [P, QUARTER], number) for k, number in enumerate((1, 5))]
@@ -191,34 +197,34 @@ def tile_picked_yldpc_bp_po_kernel(
             for t in (2, 3):
                 nc.vector.tensor_tensor(z[1][:, t - 2, nodes], picked(t, 2, nodes), part[t - 2][:], ALU.mult)
 
-        def take_logs(t, nodes, logs):
-            zs = z[t // 2][:, t % 2, nodes]
-            nc.scalar.activation(logs[:, 0, :], zs, ACT.Ln, scale=SLOPE, bias=1.0)
-            nc.scalar.activation(logs[:, 1, :], zs, ACT.Ln, scale=-SLOPE, bias=1.0)
+        def take_logs(logs, zs):
+            for s, slope in enumerate((SLOPE, -SLOPE)):
+                nc.scalar.activation(logs[:, s], zs, ACT.Ln, scale=slope, bias=1.0)
 
-        damped = [sbuf("damped%d" % c, [P, 2, PACK, CHUNK], F32) for c in range(2)]
+        damped = sbuf("damped", [P, 2, 2, PACK, CHUNK], F32)
 
-        def damp_logs(c, t, logs):
-            if t < 2:
-                nc.vector.tensor_scalar(damped[c][:, :, t, :], logs, damp_t[:, t : t + 1], None, ALU.mult)
-            else:
-                nc.scalar.activation(damped[c][:, :, t, :], logs, ACT.Copy, scale=damp_t[:, t : t + 1])
+        def damp_on_scalar(c, t, logs):
+            nc.scalar.activation(damped[:, c, :, t, :], logs, ACT.Copy, scale=damp_t[:, t : t + 1])
 
-        logs = [sbuf("logs%d" % t, [P, 2, V if t < 2 else CHUNK], F32) for t in range(PACK)]
+        def damp_on_vector(out, t, logs):
+            nc.vector.tensor_scalar(out, logs, damp_t[:, t : t + 1], None, ALU.mult)
+
+        logs = [sbuf("logs%d" % t, [P, 2, V], F32) for t in range(2)]
+        late = [sbuf("late%d" % e, [P, 2, CHUNK], F32) for e in range(2)]
         for t in (0, 1):
-            take_logs(t, both, logs[t])
-        for c in range(2):
-            for t in (0, 1):
-                damp_logs(c, t, logs[t][:, :, chunks[c]])
+            take_logs(logs[t], z[0][:, t, :])
+        for c, t in ((0, 0), (0, 1), (1, 0)):
+            damp_on_vector(damped[:, c, :, t, :], t, logs[t][:, :, chunks[c]])
         for t in (2, 3):
-            take_logs(t, chunks[0], logs[t])
+            take_logs(late[t - 2], z[1][:, t - 2, chunks[0]])
         for t in (2, 3):
-            damp_logs(0, t, logs[t][:])
-        last_logs = sbuf("last_logs", [P, 2, 2, CHUNK], F32, tag="logs2")
+            damp_on_scalar(0, t, late[t - 2][:])
+        last_logs = sbuf("last_logs", [P, 2, 2, CHUNK], F32, tag="late0")
         for t in (2, 3):
-            take_logs(t, chunks[1], last_logs[:, t - 2])
+            take_logs(last_logs[:, t - 2], z[1][:, t - 2, chunks[1]])
         for t in (2, 3):
-            damp_logs(1, t, last_logs[:, t - 2])
+            damp_on_scalar(1, t, last_logs[:, t - 2])
+        damp_on_scalar(1, 1, logs[1][:, :, chunks[1]])
 
         y_cd = sbuf("y_cd", [P, V], U32)
         y_sc = sbuf("y_sc", [P, V], U8)
@@ -233,8 +239,8 @@ def tile_picked_yldpc_bp_po_kernel(
         def subtract(c):
             nc.vector.tensor_tensor(
                 woven(rr_bf[c][:]),
-                by_fours(damped[c][:, 0]),
-                by_fours(damped[c][:, 1]),
+                by_fours(damped[:, c, 0]),
+                by_fours(damped[:, c, 1]),
                 ALU.subtract,
             )
 
@@ -257,7 +263,7 @@ def tile_picked_yldpc_bp_po_kernel(
         ]
         subtract(0)
         w2_cd = sbuf("w2_cd", [P, N], U32)
-        w2_sc = sbuf("w2_sc", [P, N], U8, tag="logs3")
+        w2_sc = sbuf("w2_sc", [P, N], U8, tag="late1")
         quantise(w2_cd[:], w2_sc[:], w2_bf[:].rearrange("p t m j -> p (t m j)"))
         for c in range(2):
             if c:

@@ -213,7 +213,7 @@ def tile_picked_yldpc_bp_po_kernel(
         late = [sbuf("late%d" % e, [P, 2, CHUNK], F32) for e in range(2)]
         for t in (0, 1):
             take_logs(logs[t], z[0][:, t, :])
-        for c, t in ((0, 0), (0, 1), (1, 0)):
+        for c, t in ((0, 0), (0, 1), (1, 0), (1, 1)):
             damp_on_vector(damped[:, c, :, t, :], t, logs[t][:, :, chunks[c]])
         for t in (2, 3):
             take_logs(late[t - 2], z[1][:, t - 2, chunks[0]])
@@ -224,7 +224,6 @@ def tile_picked_yldpc_bp_po_kernel(
             take_logs(last_logs[:, t - 2], z[1][:, t - 2, chunks[1]])
         for t in (2, 3):
             damp_on_scalar(1, t, last_logs[:, t - 2])
-        damp_on_scalar(1, 1, logs[1][:, :, chunks[1]])
 
         y_cd = sbuf("y_cd", [P, V], U32)
         y_sc = sbuf("y_sc", [P, V], U8)

@@ -21,7 +21,10 @@ STRIPE = 16
 HALF = S // 2
 QUARTER = S // 4
 CHUNK = V // 2
-SLOPE = 0.98
+QUADRANT = 32
+ROWS = 4
+CLEAR_SPLIT = 3 * T // 4
+SLOPES = (0.98, -0.98)
 
 
 def dealt_pair(raw, dealt, pair):
@@ -78,20 +81,19 @@ def tile_picked_yldpc_bp_po_kernel(
         w1_raw = sbuf("w1_raw", [P, PACK, H], F32, tag="staging")
         damp_t = sbuf("damp_t", [P, PACK], F32)
 
-        nc.vector.memset(x_sc[:, 0 : 3 * T // 4].bitcast(I32), 0)
-        nc.gpsimd.memset(x_sc[:, 3 * T // 4 : T].bitcast(I32), 0)
+        nc.vector.memset(x_sc[:, 0:CLEAR_SPLIT].bitcast(I32), 0)
+        nc.gpsimd.memset(x_sc[:, CLEAR_SPLIT:T].bitcast(I32), 0)
         nc.sync.dma_start(w1_raw[:], w1.rearrange("(p j) c -> p j c", j=PACK))
         nc.sync.dma_start(offs_t[:], offs)
-        scale_rows = x_scales[0].rearrange("(q r) c -> r q c", r=4)
-        for r in range(4):
-            nc.sync.dma_start(x_sc[r:P:32, :].bitcast(I32), scale_rows[r].bitcast(I32))
+        scale_rows = x_scales[0].rearrange("(q r) c -> r q c", r=ROWS)
+        for r in range(ROWS):
+            nc.sync.dma_start(x_sc[r:P:QUADRANT, :].bitcast(I32), scale_rows[r].bitcast(I32))
         nc.sync.dma_start(x_wd[:].bitcast(I32), x_words[0].rearrange("p n t -> p (n t)").bitcast(I32))
         w2_rows = w2.rearrange("(p j) c -> p j c", j=PACK)
         w2_early = sbuf("w2_early", [P, PACK, N // 2], F32)
         nc.sync.dma_start(w2_early[:], w2_rows[:, :, 0 : N // 2])
-        nc.sync.dma_start(pos_t[0][:], pos1)
-        nc.sync.dma_start(pos_t[1][:], pos2)
-        nc.sync.dma_start(pos_t[2][:], pos3)
+        for tile, pos in zip(pos_t, (pos1, pos2, pos3)):
+            nc.sync.dma_start(tile[:], pos)
         nc.sync.dma_start(damp_t[:], damp.rearrange("(p t) o -> p (t o)", t=PACK))
 
         xg_sc = sbuf("xg_sc", [P, S], U8)
@@ -109,11 +111,11 @@ def tile_picked_yldpc_bp_po_kernel(
 
         quantise_w1(0)
 
-        xg_wd = [sbuf("xg_wd%d" % s, [P, HALF], U32) for s in range(2)]
+        xg_wd = [sbuf("xg_wd%d" % half, [P, HALF], U32) for half in range(2)]
         for first, width in ((0, HALF), (HALF, QUARTER), (HALF + QUARTER, QUARTER)):
             entries = slice(first // STRIPE, (first + width) // STRIPE)
-            s, inside = divmod(first, HALF)
-            nc.vector.tensor_copy(xg_wd[s][:, inside : inside + width], x_wd[:].indirect(offs_t[:, entries]))
+            half, inside = divmod(first, HALF)
+            nc.vector.tensor_copy(xg_wd[half][:, inside : inside + width], x_wd[:].indirect(offs_t[:, entries]))
 
         w2_bf = sbuf("w2_bf", [P, PACK, P, PACK], BF16)
         nc.vector.tensor_copy(*dealt_all(w2_early, w2_bf[:, :, 0 : P // 2, :]))
@@ -126,13 +128,13 @@ def tile_picked_yldpc_bp_po_kernel(
 
         def product1(out, t, first, width):
             u, e = divmod(t, 2)
-            s, inside = divmod(first, HALF)
+            half, inside = divmod(first, HALF)
             group = slice(e * P, (e + 1) * P)
             product(
                 out,
                 w1_cd[u][:, group],
                 w1_sc[u][:, group],
-                xg_wd[s][:, inside : inside + width],
+                xg_wd[half][:, inside : inside + width],
                 xg_sc[:, first : first + width],
             )
 
@@ -173,55 +175,52 @@ def tile_picked_yldpc_bp_po_kernel(
         def picked(t, d, nodes):
             return h[t][:].indirect(pos_t[d][:, nodes.start // STRIPE : nodes.stop // STRIPE])
 
-        def factor1(t, nodes):
-            if t < 2:
-                nc.vector.tensor_copy(one[t][:, nodes], picked(t, 0, nodes))
-            else:
-                nc.scalar.activation(one[t][:, nodes], picked(t, 0, nodes), ACT.Copy)
+        def times_picked(out, t, d, nodes, factor):
+            nc.vector.tensor_tensor(out, picked(t, d, nodes), factor, ALU.mult)
 
-        def factor2(t, nodes):
-            nc.vector.tensor_tensor(two[t][:, nodes], picked(t, 1, nodes), one[t][:, nodes], ALU.mult)
-
-        def factor3(t, nodes):
-            nc.vector.tensor_tensor(z[t // 2][:, t % 2, nodes], picked(t, 2, nodes), two[t][:, nodes], ALU.mult)
-
-        for t in range(PACK):
-            factor1(t, both)
-        for factor in (factor2, factor3):
-            for t in (0, 1):
-                factor(t, both)
+        for t in (0, 1):
+            nc.vector.tensor_copy(one[t][:], picked(t, 0, both))
+        for t in (2, 3):
+            nc.scalar.activation(one[t][:], picked(t, 0, both), ACT.Copy)
+        for t in (0, 1):
+            times_picked(two[t][:], t, 1, both, one[t][:])
+        for t in (0, 1):
+            times_picked(z[0][:, t], t, 2, both, two[t][:])
         for nodes in chunks:
             part = [sbuf("part%d_%d" % (t, nodes.start), [P, CHUNK], F32, tag="part%d" % t) for t in (2, 3)]
             for t in (2, 3):
-                nc.vector.tensor_tensor(part[t - 2][:], picked(t, 1, nodes), one[t][:, nodes], ALU.mult)
+                times_picked(part[t - 2][:], t, 1, nodes, one[t][:, nodes])
             for t in (2, 3):
-                nc.vector.tensor_tensor(z[1][:, t - 2, nodes], picked(t, 2, nodes), part[t - 2][:], ALU.mult)
-
-        def take_logs(logs, zs):
-            for s, slope in enumerate((SLOPE, -SLOPE)):
-                nc.scalar.activation(logs[:, s], zs, ACT.Ln, scale=slope, bias=1.0)
+                times_picked(z[1][:, t - 2, nodes], t, 2, nodes, part[t - 2][:])
 
         damped = sbuf("damped", [P, 2, 2, PACK, CHUNK], F32)
+
+        def take_log(out, zs, sign):
+            nc.scalar.activation(out, zs, ACT.Ln, scale=SLOPES[sign], bias=1.0)
 
         def damp_on_scalar(c, t, logs):
             nc.scalar.activation(damped[:, c, :, t, :], logs, ACT.Copy, scale=damp_t[:, t : t + 1])
 
-        def damp_on_vector(out, t, logs):
-            nc.vector.tensor_scalar(out, logs, damp_t[:, t : t + 1], None, ALU.mult)
+        def damp_on_vector(c, t, logs):
+            nc.vector.tensor_scalar(damped[:, c, :, t, :], logs, damp_t[:, t : t + 1], None, ALU.mult)
 
-        logs = [sbuf("logs%d" % t, [P, 2, V], F32) for t in range(2)]
-        late = [sbuf("late%d" % e, [P, 2, CHUNK], F32) for e in range(2)]
+        early_logs = sbuf("early_logs", [P, 2, 2, V], F32)
         for t in (0, 1):
-            take_logs(logs[t], z[0][:, t, :])
-        for c, t in ((0, 0), (0, 1), (1, 0), (1, 1)):
-            damp_on_vector(damped[:, c, :, t, :], t, logs[t][:, :, chunks[c]])
+            take_log(early_logs[:, t, 0], z[0][:, t], 0)
+        take_log(early_logs[:, :, 1], z[0][:], 1)
+        for c in range(2):
+            for t in (0, 1):
+                damp_on_vector(c, t, early_logs[:, t, :, chunks[c]])
+        late_logs = [sbuf("late_logs%d" % t, [P, 2, CHUNK], F32) for t in (2, 3)]
         for t in (2, 3):
-            take_logs(late[t - 2], z[1][:, t - 2, chunks[0]])
+            for sign in range(2):
+                take_log(late_logs[t - 2][:, sign], z[1][:, t - 2, chunks[0]], sign)
         for t in (2, 3):
-            damp_on_scalar(0, t, late[t - 2][:])
-        last_logs = sbuf("last_logs", [P, 2, 2, CHUNK], F32, tag="late0")
+            damp_on_scalar(0, t, late_logs[t - 2][:])
+        last_logs = sbuf("last_logs", [P, 2, 2, CHUNK], F32, tag="late_logs2")
+        take_log(last_logs[:, :, 1], z[1][:, :, chunks[1]], 1)
         for t in (2, 3):
-            take_logs(last_logs[:, t - 2], z[1][:, t - 2, chunks[1]])
+            take_log(last_logs[:, t - 2, 0], z[1][:, t - 2, chunks[1]], 0)
         for t in (2, 3):
             damp_on_scalar(1, t, last_logs[:, t - 2])
 
@@ -262,7 +261,7 @@ def tile_picked_yldpc_bp_po_kernel(
         ]
         subtract(0)
         w2_cd = sbuf("w2_cd", [P, N], U32)
-        w2_sc = sbuf("w2_sc", [P, N], U8, tag="late1")
+        w2_sc = sbuf("w2_sc", [P, N], U8, tag="late_logs3")
         quantise(w2_cd[:], w2_sc[:], w2_bf[:].rearrange("p t m j -> p (t m j)"))
         for c in range(2):
             if c:
@@ -278,8 +277,7 @@ def tile_picked_yldpc_bp_po_kernel(
         out_words = out_1[0].rearrange("p n t -> p (n t)").bitcast(I32)
         for c, queue in enumerate((nc.scalar, nc.sync)):
             queue.dma_start(out_words[:, chunks[c]], y_cd[:, chunks[c]].bitcast(I32))
-        for q in range(4):
+        for q in range(P // QUADRANT):
             queue = nc.sync if q % 2 else nc.scalar
-            queue.dma_start(
-                out_2[0, 4 * q : 4 * q + 4, :].bitcast(I32), y_sc[32 * q : 32 * q + 4, :].bitcast(I32)
-            )
+            rows = out_2[0, ROWS * q : ROWS * (q + 1), :]
+            queue.dma_start(rows.bitcast(I32), y_sc[QUADRANT * q : QUADRANT * q + ROWS, :].bitcast(I32))

@@ -24,6 +24,7 @@ CHUNK = V // 2
 QUADRANT = 32
 ROWS = 4
 CLEAR_SPLIT = 3 * T // 4
+HALF_BANKS = ((1, (2, 6)), (2, (3, 4)), (3, (7, 0)))
 SLOPES = (0.98, -0.98)
 
 
@@ -101,7 +102,7 @@ def tile_picked_yldpc_bp_po_kernel(
 
         w1_bf = [sbuf("w1_bf%d" % u, [P, 2, P, PACK], BF16) for u in range(2)]
         w1_cd = [sbuf("w1_cd%d" % u, [P, 2 * P], U32, tag=tag) for u, tag in enumerate(("", "x_wd"))]
-        w1_planes = sbuf("w1_planes", [P, PACK * P], U8, tag="x_sc")
+        w1_planes = sbuf("w1_planes", [P, PACK * P], U8)
         w1_sc = [w1_planes[:, 2 * P * u : 2 * P * (u + 1)] for u in range(2)]
         nc.vector.tensor_copy(*dealt_pair(w1_raw, w1_bf[0], 0))
         nc.scalar.activation(*dealt_pair(w1_raw, w1_bf[1], 1), ACT.Copy)
@@ -123,7 +124,7 @@ def tile_picked_yldpc_bp_po_kernel(
 
         head = bank("head", [P, HALF], 0)
         ends = [bank("end%d" % k, [P, QUARTER], number) for k, number in enumerate((1, 5))]
-        rest = [bank("rest%d" % t, [P, S], t + 1) for t in range(1, PACK)]
+        halves = [[bank("half%d%d" % (t, k), [P, HALF], numbers[k]) for k in range(2)] for t, numbers in HALF_BANKS]
         h = [sbuf("h%d" % t, [P, S], F32) for t in range(PACK)]
 
         def product1(out, t, first, width):
@@ -141,19 +142,21 @@ def tile_picked_yldpc_bp_po_kernel(
         def tanh_half(out, sums):
             nc.scalar.activation(out, sums, ACT.Tanh, scale=0.5)
 
+        def half_group(t, k):
+            product1(halves[t - 1][k][:], t, k * HALF, HALF)
+            tanh_half(h[t][:, k * HALF : (k + 1) * HALF], halves[t - 1][k][:])
+
         product1(head[:], 0, 0, HALF)
         tanh_half(h[0][:, 0:HALF], head[:])
-        product1(rest[0][:, 0:HALF], 1, 0, HALF)
+        half_group(1, 0)
         for k in range(2):
             first = HALF + k * QUARTER
             product1(ends[k][:], 0, first, QUARTER)
             tanh_half(h[0][:, first : first + QUARTER], ends[k][:])
-        product1(rest[0][:, HALF:S], 1, HALF, HALF)
-        tanh_half(h[1][:], rest[0][:])
+        half_group(1, 1)
         for t in (2, 3):
-            for first in (0, HALF):
-                product1(rest[t - 1][:, first : first + HALF], t, first, HALF)
-            tanh_half(h[t][:], rest[t - 1][:])
+            for k in range(2):
+                half_group(t, k)
 
         w2_late = sbuf("w2_late", [P, PACK, N // 2], F32, tag="staging")
         nc.sync.dma_start(w2_late[:], w2_rows[:, :, N // 2 : N])

@@ -25,6 +25,7 @@ QUADRANT = 32
 ROWS = 4
 CLEAR_SPLIT = 3 * T // 4
 HALF_BANKS = ((1, (2, 6)), (2, (3, 4)), (3, (7, 0)))
+EARLY = 320
 SLOPES = (0.98, -0.98)
 
 
@@ -91,8 +92,8 @@ def tile_picked_yldpc_bp_po_kernel(
             nc.sync.dma_start(x_sc[r:P:QUADRANT, :].bitcast(I32), scale_rows[r].bitcast(I32))
         nc.sync.dma_start(x_wd[:].bitcast(I32), x_words[0].rearrange("p n t -> p (n t)").bitcast(I32))
         w2_rows = w2.rearrange("(p j) c -> p j c", j=PACK)
-        w2_early = sbuf("w2_early", [P, PACK, N // 2], F32)
-        nc.sync.dma_start(w2_early[:], w2_rows[:, :, 0 : N // 2])
+        w2_early = sbuf("w2_early", [P, PACK, EARLY], F32)
+        nc.sync.dma_start(w2_early[:], w2_rows[:, :, 0:EARLY])
         for tile, pos in zip(pos_t, (pos1, pos2, pos3)):
             nc.sync.dma_start(tile[:], pos)
         nc.sync.dma_start(damp_t[:], damp.rearrange("(p t) o -> p (t o)", t=PACK))
@@ -119,7 +120,7 @@ def tile_picked_yldpc_bp_po_kernel(
             nc.vector.tensor_copy(xg_wd[half][:, inside : inside + width], x_wd[:].indirect(offs_t[:, entries]))
 
         w2_bf = sbuf("w2_bf", [P, PACK, P, PACK], BF16)
-        nc.vector.tensor_copy(*dealt_all(w2_early, w2_bf[:, :, 0 : P // 2, :]))
+        nc.vector.tensor_copy(*dealt_all(w2_early, w2_bf[:, :, 0 : EARLY // PACK, :]))
         quantise_w1(1)
 
         head = bank("head", [P, HALF], 0)
@@ -158,10 +159,10 @@ def tile_picked_yldpc_bp_po_kernel(
             for k in range(2):
                 half_group(t, k)
 
-        w2_late = sbuf("w2_late", [P, PACK, N // 2], F32, tag="staging")
-        nc.sync.dma_start(w2_late[:], w2_rows[:, :, N // 2 : N])
+        w2_late = sbuf("w2_late", [P, PACK, N - EARLY], F32, tag="staging")
+        nc.sync.dma_start(w2_late[:], w2_rows[:, :, EARLY:N])
         nc.gpsimd.tensor_scalar(
-            w2_bf[:, :, P // 2 : P, :].rearrange("p t m j -> p m t j"),
+            w2_bf[:, :, EARLY // PACK : P, :].rearrange("p t m j -> p m t j"),
             w2_late[:].rearrange("p j (m t) -> p m t j", t=PACK),
             1.0,
             0.0,
@@ -221,9 +222,9 @@ def tile_picked_yldpc_bp_po_kernel(
         for t in (2, 3):
             damp_on_scalar(0, t, late_logs[t - 2][:])
         last_logs = sbuf("last_logs", [P, 2, 2, CHUNK], F32, tag="late_logs2")
-        take_log(last_logs[:, :, 1], z[1][:, :, chunks[1]], 1)
         for t in (2, 3):
-            take_log(last_logs[:, t - 2, 0], z[1][:, t - 2, chunks[1]], 0)
+            for sign in range(2):
+                take_log(last_logs[:, t - 2, sign], z[1][:, t - 2, chunks[1]], sign)
         for t in (2, 3):
             damp_on_scalar(1, t, last_logs[:, t - 2])
 

from contextlib import ExitStack

import concourse.mybir as mybir

K, T, S, V, H, N = 512, 2048, 512, 256, 512, 512
FLOPS = 2 * K * H * S + 2 * H * N * V

F32 = mybir.dt.float32
BF16 = mybir.dt.bfloat16
I32 = mybir.dt.int32
U32 = mybir.dt.uint32
U16 = mybir.dt.uint16
U8 = mybir.dt.uint8
FP8X4 = mybir.dt.float8_e4m3fn_x4
ACT = mybir.ActivationFunctionType
ALU = mybir.AluOpType

P = 128
PACK = 4
STRIPE = 16
HALF = S // 2
QUARTER = S // 4
CHUNK = V // 2
QUADRANT = 32
ROWS = 4
CLEAR_SPLIT = 3 * T // 4
HALF_BANKS = ((1, (2, 6)), (2, (3, 4)), (3, (7, 0)))
EARLY = 320
SLOPES = (0.98, -0.98)


def dealt_pair(raw, dealt, pair):
    src = raw[:].rearrange("p j (m t) -> p m j t", t=PACK)[:, :, :, 2 * pair : 2 * pair + 2]
    return dealt[:].rearrange("p t m j -> p m j t"), src


def dealt_all(raw, dealt):
    return dealt.rearrange("p t m j -> p m j t"), raw[:].rearrange("p j (m t) -> p m j t", t=PACK)


def by_fours(grouped):
    return grouped.rearrange("p t (g i) -> p g t i", i=4)


def woven(tile):
    return tile.rearrange("p (g i) t -> p g t i", i=4)


def tile_picked_yldpc_bp_po_kernel(
    tc, x_words, x_scales, w1, w2, damp, offs, pos1, pos2, pos3, out_0, out_1, out_2
):
    nc = tc.nc
    with ExitStack() as ctx:
        lists = ctx.enter_context(tc.tile_pool(name="lists", bufs=1))
        keep = ctx.enter_context(tc.tile_pool(name="keep", bufs=1))
        psum = ctx.enter_context(tc.psum_pool(name="psum", bufs=1))

        def sbuf(name, shape, dtype, tag=""):
            return keep.tile(shape, dtype, name=name, tag=tag or name, align_bytes=64)

        def bank(name, shape, number):
            return psum.tile(shape, F32, name=name, tag="bank%d" % number)

        def quantise(codes, scales, values):
            nc.vector.quantize_mx(out=codes.bitcast(FP8X4), scales=scales, in_=values)

        def product(out, w_codes, w_scales, codes, scales):
            nc.tensor.matmul_mx(
                out=out,
                lhsT=w_codes.bitcast(FP8X4),
                lhsT_scale=w_scales,
                rhs=codes.bitcast(FP8X4),
                rhs_scale=scales,
                start=True,
                stop=True,
            )

        offs_t = lists.tile([P, S // STRIPE], U16, name="offs_t")
        pos_t = [lists.tile([P, V // STRIPE], U16, name="pos_t%d" % d) for d in range(3)]

        x_sc = sbuf("x_sc", [P, T], U8)
        x_wd = sbuf("x_wd", [P, T], U32)
        w1_raw = sbuf("w1_raw", [P, PACK, H], F32, tag="staging")
        damp_t = sbuf("damp_t", [P, PACK], F32)

        nc.vector.memset(x_sc[:, 0:CLEAR_SPLIT].bitcast(I32), 0)
        nc.gpsimd.memset(x_sc[:, CLEAR_SPLIT:T].bitcast(I32), 0)
        nc.sync.dma_start(w1_raw[:], w1.rearrange("(p j) c -> p j c", j=PACK))
        nc.sync.dma_start(offs_t[:], offs)
        scale_rows = x_scales[0].rearrange("(q r) c -> r q c", r=ROWS)
        for r in range(ROWS):
            nc.sync.dma_start(x_sc[r:P:QUADRANT, :].bitcast(I32), scale_rows[r].bitcast(I32))
        nc.sync.dma_start(x_wd[:].bitcast(I32), x_words[0].rearrange("p n t -> p (n t)").bitcast(I32))
        w2_rows = w2.rearrange("(p j) c -> p j c", j=PACK)
        w2_early = sbuf("w2_early", [P, PACK, EARLY], F32)
        nc.sync.dma_start(w2_early[:], w2_rows[:, :, 0:EARLY])
        for tile, pos in zip(pos_t, (pos1, pos2, pos3)):
            nc.sync.dma_start(tile[:], pos)
        nc.sync.dma_start(damp_t[:], damp.rearrange("(p t) o -> p (t o)", t=PACK))

        xg_sc = sbuf("xg_sc", [P, S], U8)
        nc.vector.tensor_copy(xg_sc[:], x_sc[:].indirect(offs_t[:]))

        w1_bf = [sbuf("w1_bf%d" % u, [P, 2, P, PACK], BF16) for u in range(2)]
        w1_cd = [sbuf("w1_cd%d" % u, [P, 2 * P], U32, tag=tag) for u, tag in enumerate(("", "x_wd"))]
        w1_planes = sbuf("w1_planes", [P, PACK * P], U8)
        w1_sc = [w1_planes[:, 2 * P * u : 2 * P * (u + 1)] for u in range(2)]
        nc.vector.tensor_copy(*dealt_pair(w1_raw, w1_bf[0], 0))
        nc.scalar.activation(*dealt_pair(w1_raw, w1_bf[1], 1), ACT.Copy)

        def quantise_w1(u):
            quantise(w1_cd[u][:], w1_sc[u], w1_bf[u][:].rearrange("p t m j -> p (t m j)"))

        quantise_w1(0)

        xg_wd = [sbuf("xg_wd%d" % half, [P, HALF], U32) for half in range(2)]
        for first, width in ((0, HALF), (HALF, QUARTER), (HALF + QUARTER, QUARTER)):
            entries = slice(first // STRIPE, (first + width) // STRIPE)
            half, inside = divmod(first, HALF)
            nc.vector.tensor_copy(xg_wd[half][:, inside : inside + width], x_wd[:].indirect(offs_t[:, entries]))

        w2_bf = sbuf("w2_bf", [P, PACK, P, PACK], BF16)
        nc.vector.tensor_copy(*dealt_all(w2_early, w2_bf[:, :, 0 : EARLY // PACK, :]))
        quantise_w1(1)

        head = bank("head", [P, HALF], 0)
        ends = [bank("end%d" % k, [P, QUARTER], number) for k, number in enumerate((1, 5))]
        halves = [[bank("half%d%d" % (t, k), [P, HALF], numbers[k]) for k in range(2)] for t, numbers in HALF_BANKS]
        h = [sbuf("h%d" % t, [P, S], F32) for t in range(PACK)]

        def product1(out, t, first, width):
            u, e = divmod(t, 2)
            half, inside = divmod(first, HALF)
            group = slice(e * P, (e + 1) * P)
            product(
                out,
                w1_cd[u][:, group],
                w1_sc[u][:, group],
                xg_wd[half][:, inside : inside + width],
                xg_sc[:, first : first + width],
            )

        def tanh_half(out, sums):
            nc.scalar.activation(out, sums, ACT.Tanh, scale=0.5)

        def half_group(t, k):
            product1(halves[t - 1][k][:], t, k * HALF, HALF)
            tanh_half(h[t][:, k * HALF : (k + 1) * HALF], halves[t - 1][k][:])

        product1(head[:], 0, 0, HALF)
        tanh_half(h[0][:, 0:HALF], head[:])
        half_group(1, 0)
        for k in range(2):
            first = HALF + k * QUARTER
            product1(ends[k][:], 0, first, QUARTER)
            tanh_half(h[0][:, first : first + QUARTER], ends[k][:])
        half_group(1, 1)
        for t in (2, 3):
            for k in range(2):
                half_group(t, k)

        w2_late = sbuf("w2_late", [P, PACK, N - EARLY], F32, tag="staging")
        nc.sync.dma_start(w2_late[:], w2_rows[:, :, EARLY:N])
        nc.gpsimd.tensor_scalar(
            w2_bf[:, :, EARLY // PACK : P, :].rearrange("p t m j -> p m t j"),
            w2_late[:].rearrange("p j (m t) -> p m t j", t=PACK),
            1.0,
            0.0,
            ALU.mult,
            ALU.add,
        )

        one = [sbuf("one%d" % t, [P, V], F32) for t in range(PACK)]
        two = [sbuf("two%d" % t, [P, V], F32) for t in range(2)]
        z = [sbuf("z%d" % u, [P, 2, V], F32) for u in range(2)]
        chunks = [slice(c * CHUNK, (c + 1) * CHUNK) for c in range(2)]
        both = slice(0, V)

        def picked(t, d, nodes):
            return h[t][:].indirect(pos_t[d][:, nodes.start // STRIPE : nodes.stop // STRIPE])

        def times_picked(out, t, d, nodes, factor):
            nc.vector.tensor_tensor(out, picked(t, d, nodes), factor, ALU.mult)

        for t in (0, 1):
            nc.vector.tensor_copy(one[t][:], picked(t, 0, both))
        for t in (2, 3):
            nc.scalar.activation(one[t][:], picked(t, 0, both), ACT.Copy)
        for t in (0, 1):
            times_picked(two[t][:], t, 1, both, one[t][:])
        for t in (0, 1):
            times_picked(z[0][:, t], t, 2, both, two[t][:])
        for nodes in chunks:
            part = [sbuf("part%d_%d" % (t, nodes.start), [P, CHUNK], F32, tag="part%d" % t) for t in (2, 3)]
            for t in (2, 3):
                times_picked(part[t - 2][:], t, 1, nodes, one[t][:, nodes])
            for t in (2, 3):
                times_picked(z[1][:, t - 2, nodes], t, 2, nodes, part[t - 2][:])

        damped = sbuf("damped", [P, 2, 2, PACK, CHUNK], F32)

        def take_log(out, zs, sign):
            nc.scalar.activation(out, zs, ACT.Ln, scale=SLOPES[sign], bias=1.0)

        def damp_on_scalar(c, t, logs):
            nc.scalar.activation(damped[:, c, :, t, :], logs, ACT.Copy, scale=damp_t[:, t : t + 1])

        def damp_on_vector(c, t, logs):
            nc.vector.tensor_scalar(damped[:, c, :, t, :], logs, damp_t[:, t : t + 1], None, ALU.mult)

        early_logs = sbuf("early_logs", [P, 2, 2, V], F32)
        for t in (0, 1):
            take_log(early_logs[:, t, 0], z[0][:, t], 0)
        take_log(early_logs[:, :, 1], z[0][:], 1)
        for c in range(2):
            for t in (0, 1):
                damp_on_vector(c, t, early_logs[:, t, :, chunks[c]])
        late_logs = [sbuf("late_logs%d" % t, [P, 2, CHUNK], F32) for t in (2, 3)]
        for t in (2, 3):
            for sign in range(2):
                take_log(late_logs[t - 2][:, sign], z[1][:, t - 2, chunks[0]], sign)
        for t in (2, 3):
            damp_on_scalar(0, t, late_logs[t - 2][:])
        last_logs = sbuf("last_logs", [P, 2, 2, CHUNK], F32, tag="late_logs2")
        for t in (2, 3):
            for sign in range(2):
                take_log(last_logs[:, t - 2, sign], z[1][:, t - 2, chunks[1]], sign)
        for t in (2, 3):
            damp_on_scalar(1, t, last_logs[:, t - 2])

        y_cd = sbuf("y_cd", [P, V], U32)
        y_sc = sbuf("y_sc", [P, V], U8)
        out_rows = out_0.rearrange("(p t) v -> p t v", t=PACK)
        rr_bf = [sbuf("rr_bf%d" % c, [P, CHUNK, PACK], BF16) for c in range(2)]
        rr_cd = [sbuf("rr_cd%d" % c, [P, CHUNK], U32) for c in range(2)]
        rr_sc = [sbuf("rr_sc%d" % c, [P, CHUNK], U8) for c in range(2)]
        y = [sbuf("y%d" % c, [P, PACK, CHUNK], F32) for c in range(2)]
        y_bf = [sbuf("y_bf%d" % c, [P, CHUNK, PACK], BF16) for c in range(2)]
        pairs = [slice(0, 2), slice(2, 4)]

        def subtract(c):
            nc.vector.tensor_tensor(
                woven(rr_bf[c][:]),
                by_fours(damped[:, c, 0]),
                by_fours(damped[:, c, 1]),
                ALU.subtract,
            )

        def quantise_rr(c):
            quantise(rr_cd[c][:], rr_sc[c][:], rr_bf[c][:].rearrange("p v t -> p (v t)"))

        def product2(c, groups, number, leave):
            sums = bank("acc%d%d" % (c, groups.start), [P, groups.stop - groups.start, CHUNK], number)
            for t in range(groups.start, groups.stop):
                group = slice(t * P, (t + 1) * P)
                product(sums[:, t - groups.start, :], w2_cd[:, group], w2_sc[:, group], rr_cd[c][:], rr_sc[c][:])
            leave(y[c][:, groups, :], sums[:])

        def by_scalar(out, sums):
            nc.scalar.activation(out, sums, ACT.Copy)

        ways_out = [
            [(pairs[0], 5, by_scalar), (pairs[1], 6, by_scalar)],
            [(pairs[0], 7, nc.vector.tensor_copy), (slice(2, 3), 0, by_scalar), (slice(3, 4), 1, by_scalar)],
        ]
        subtract(0)
        w2_cd = sbuf("w2_cd", [P, N], U32)
        w2_sc = sbuf("w2_sc", [P, N], U8, tag="late_logs3")
        quantise(w2_cd[:], w2_sc[:], w2_bf[:].rearrange("p t m j -> p (t m j)"))
        for c in range(2):
            if c:
                subtract(c)
            quantise_rr(c)
            for way in ways_out[c]:
                product2(c, *way)
            nc.sync.dma_start(out_rows[:, :, chunks[c]], y[c][:])

        for c in range(2):
            nc.vector.tensor_copy(woven(y_bf[c][:]), by_fours(y[c][:]))
            quantise(y_cd[:, chunks[c]], y_sc[:, chunks[c]], y_bf[c][:].rearrange("p v t -> p (v t)"))
        out_words = out_1[0].rearrange("p n t -> p (n t)").bitcast(I32)
        for c, queue in enumerate((nc.scalar, nc.sync)):
            queue.dma_start(out_words[:, chunks[c]], y_cd[:, chunks[c]].bitcast(I32))
        for q in range(P // QUADRANT):
            queue = nc.sync if q % 2 else nc.scalar
            rows = out_2[0, ROWS * q : ROWS * (q + 1), :]
            queue.dma_start(rows.bitcast(I32), y_sc[QUADRANT * q : QUADRANT * q + ROWS, :].bitcast(I32))
